import numpy as np
import ml_dtypes


def mxq(x, axis, fmt="e4m3"):
    dtype, down = {"e4m3": (ml_dtypes.float8_e4m3fn, 7), "e5m2": (ml_dtypes.float8_e5m2, 14)}[fmt]
    v = np.moveaxis(np.asarray(x, np.float32).astype(ml_dtypes.bfloat16).astype(np.float64), axis, -1)
    blocks = v.reshape(v.shape[:-1] + (-1, 32))
    amax = np.abs(blocks).max(-1, keepdims=True)
    byte = np.maximum(np.where(amax > 0, np.frexp(amax)[1] - 1 + 127, 0) - down, 1)
    scale = np.exp2(byte - 127.0)
    codes = (blocks / scale).astype(np.float32).astype(dtype).astype(np.float64)
    return np.moveaxis((codes * scale).reshape(v.shape), -1, axis)


WIDE = False


def mx_kscale(k):
    if not WIDE:
        return np.ones(k)
    levels = np.array([24, -24, 12, -12, 0])
    if k % 512:
        return np.exp2(np.random.permutation(np.resize(levels, k // 32))).repeat(32)
    a = np.empty((k // 512, 16))
    for p in range(k // 512):
        a[p, :8] = np.random.permutation(np.resize(levels, 8))
        for g in range(8):
            far = levels[np.abs(levels - a[p, g]) >= 10]
            a[p, g + 8] = far[np.random.randint(len(far))]
    return np.exp2(a.ravel()).repeat(32)


def f64(x):
    return np.asarray(x).astype(np.float64)


def striped(idx):
    return np.tile(idx.reshape(-1, 16).T, (8, 1)).astype(np.uint16)


def unstriped(offs):
    return offs[:16].T.reshape(-1).astype(np.int64)


E2M1 = np.array([0.0, 0.5, 1.0, 1.5, 2.0, 3.0, 4.0, 6.0, -0.0, -0.5, -1.0, -1.5, -2.0, -3.0, -4.0, -6.0])


def pack_weight(w, fmt):
    k, n = w.shape
    w = f64(np.asarray(w, np.float32).astype(ml_dtypes.bfloat16)).reshape(k // 32, 32, n)
    amax = np.abs(w).max(1)
    if fmt == "e4m3":
        byte = np.frexp(amax)[1] - 1 + 127 - 7
    else:
        mant, ex = np.frexp(amax / 6.0)
        byte = np.where(mant > 0.5, ex, ex - 1) + 127
    byte = np.clip(np.where(amax > 0, byte, 1), 1, 254)
    scaled = (w * np.exp2(127.0 - byte)[:, None, :]).reshape(k, n).astype(np.float32)
    by_word = np.ascontiguousarray(scaled.reshape(k // 512, 128, 4, n).transpose(0, 1, 3, 2))
    if fmt == "e4m3":
        words = by_word.astype(ml_dtypes.float8_e4m3fn).view(np.uint8)
    else:
        c = by_word.astype(ml_dtypes.float4_e2m1fn).view(np.uint8) & 0xF
        words = (c[..., 0::2] | (c[..., 1::2] << 4)).reshape(k // 512, 128, 2 * n)
    return np.ascontiguousarray(words), np.ascontiguousarray(byte.astype(np.uint8).reshape(k // 512, 16, n))


def unpack_weight(words, scales, fmt):
    g, _, n = scales.shape
    words = np.ascontiguousarray(words).reshape(g, 128, n, -1)
    if fmt == "e4m3":
        vals = words.view(ml_dtypes.float8_e4m3fn).astype(np.float64)
    else:
        nib = np.empty((g, 128, n, 4), np.uint8)
        nib[..., 0::2] = words & 0xF
        nib[..., 1::2] = words >> 4
        vals = E2M1[nib]
    vals = vals * np.repeat(np.exp2(scales.astype(np.float64) - 127.0), 8, axis=1)[..., None]
    return vals.transpose(0, 1, 3, 2).reshape(g * 512, n)


K, R, M, N, T, J = 1024, 1024, 512, 512, 4096, 1024


def setup_inputs():
    n = np.random.standard_normal
    s = mx_kscale(K)[:, None]
    s2 = mx_kscale(K)[:, None]
    u = mx_kscale(R)[:, None]
    p_tab = pack_weight(n((K, T)) * s2, "e4m3")
    p_wq = pack_weight(n((K, R)) / np.sqrt(K) / s / u.T, "e4m3")
    p_wk = pack_weight(n((K, R)) / np.sqrt(K) / s2 * u.T, "e2m1")
    p_wv4 = pack_weight(n((K, N)) / np.sqrt(K) / s2, "e2m1")
    return {
        "tab_words": p_tab[0],
        "tab_scales": p_tab[1],
        "x": (n((K, M)) * s).astype(np.float32),
        "wq_words": p_wq[0],
        "wq_scales": p_wq[1],
        "wk_words": p_wk[0],
        "wk_scales": p_wk[1],
        "wv4_words": p_wv4[0],
        "wv4_scales": p_wv4[1],
        "wvd": (0.4 * (n((K, N)) / np.sqrt(K) / s2)).astype(np.float32),
        "offs": striped(np.random.permutation(T)[:J]),
    }


def reference(tab_words, tab_scales, x, wq_words, wq_scales, wk_words, wk_scales, wv4_words, wv4_scales, wvd, offs):
    idx = unstriped(offs)
    tab_ = unpack_weight(tab_words, tab_scales, "e4m3")[:, idx]
    x_ = mxq(f64(x), 0, "e4m3")
    wq_ = unpack_weight(wq_words, wq_scales, "e4m3")
    wk_ = unpack_weight(wk_words, wk_scales, "e2m1")
    qr = wq_.T @ x_
    kr = wk_.T @ tab_
    qr_ = mxq(qr, 0, "e4m3")
    kr_ = mxq(kr, 0, "e4m3")
    sc = qr_.T @ kr_
    wv4_ = unpack_weight(wv4_words, wv4_scales, "e2m1")
    wvd_ = mxq(f64(wvd), 0, "e4m3")
    vv = wv4_.T @ tab_ + wvd_.T @ tab_
    return sc * 0.03125, vv

@@ -1,0 +1,255 @@
+from contextlib import ExitStack
+
+import concourse.mybir as mybir
+
+K, R, M, N, T, J = 1024, 1024, 512, 512, 4096, 1024
+FLOPS = 2 * K * R * M + 2 * K * R * J + 2 * R * M * J + 4 * K * N * J
+
+F32 = mybir.dt.float32
+BF16 = mybir.dt.bfloat16
+I32 = mybir.dt.int32
+U32 = mybir.dt.uint32
+U16 = mybir.dt.uint16
+U8 = mybir.dt.uint8
+FP8X4 = mybir.dt.float8_e4m3fn_x4
+FP4X4 = mybir.dt.float4_e2m1fn_x4
+MULT = mybir.AluOpType.mult
+
+P = 128
+PACK = 4
+PASSES = 2
+BANK = 512
+HALVES = J // BANK
+QUADS = 4
+SCORE_SCALE = 0.03125
+AL = 64
+
+
+def tile_list_kvt_dl_scale_kernel(tc, tab_words, tab_scales, x, wq_words, wq_scales, wk_words, wk_scales,
+        wv4_words, wv4_scales, wvd, offs, out_0, out_1):
+    nc = tc.nc
+    with ExitStack() as ctx:
+        held = ctx.enter_context(tc.tile_pool(name="held", bufs=1))
+        keep = ctx.enter_context(tc.tile_pool(name="keep", bufs=1))
+        ring = ctx.enter_context(tc.tile_pool(name="ring", bufs=2))
+        outs = ctx.enter_context(tc.tile_pool(name="outs", bufs=6))
+        psum = ctx.enter_context(tc.psum_pool(name="psum", bufs=4))
+
+        offsets = held.tile([P, J // 16], U16, name="offsets")
+        nc.sync.dma_start(offsets[:], offs)
+
+        def tile(name, shape, dtype, tag=None):
+            return keep.tile(shape, dtype, name=name, tag=tag or name, align_bytes=AL)
+
+        def zero(engine, t):
+            engine.memset(t.bitcast(I32), 0)
+
+        def load_rows(dst, src):
+            nc.sync.dma_start(dst.bitcast(I32), src.rearrange("a q w -> q a w").bitcast(I32))
+
+        def spread_rows(queue, planes, staged):
+            for q in range(QUADS):
+                queue.dma_start(planes[32 * q : 32 * q + 4].bitcast(I32), staged[8 * q : 8 * q + 8, :].bitcast(I32))
+
+        def deal(dst, src, run):
+            nc.vector.tensor_copy(
+                dst.bitcast(I32).rearrange("p (b t g w) -> p b t g w", t=PACK, g=16, w=run),
+                src.bitcast(I32).rearrange("p (b g t w) -> p b t g w", t=PACK, g=16, w=run))
+
+        tab_s = tile("tab_s", [P, T], U8)
+        load_rows(tab_s[0:32, :], tab_scales)
+        wk_s_raw = tile("wk_s_raw", [32, R], U8)
+        load_rows(wk_s_raw[:], wk_scales)
+        wq_s_raw = tile("wq_s_raw", [32, R], U8)
+        load_rows(wq_s_raw[:], wq_scales)
+        late_rows = tile("late_rows", [32, R + N], U8)
+        load_rows(late_rows[:, R:], wv4_scales)
+        wk_raw = tile("wk_raw", [P, PASSES, 2 * R], U8, tag="slot_w")
+        nc.sync.dma_start(wk_raw[:].bitcast(I32), wk_words.rearrange("a p w -> p a w").bitcast(I32))
+        tab_w = []
+        for a in range(PASSES):
+            t = tile("tab_w%d" % a, [P, T], I32, tag="slot_tw%d" % a)
+            nc.sync.dma_start(t[:], tab_words[a].rearrange("p t i -> p (t i)").bitcast(I32))
+            tab_w.append(t)
+        wv4_c = tile("wv4_c", [P, PASSES, 2 * N], U8)
+        nc.sync.dma_start(wv4_c[:].bitcast(I32), wv4_words.rearrange("a p w -> p a w").bitcast(I32))
+
+        zero(nc.vector, tab_s[32:64, :])
+        zero(nc.vector, tab_s[64:128, :])
+        early_planes = tile("early_planes", [P, PASSES, J + R], U8)
+        zero(nc.vector, early_planes[:].rearrange("p a w -> p (a w)"))
+        late_planes = tile("late_planes", [P, PASSES, R + N], U8)
+        zero(nc.gpsimd, late_planes[:].rearrange("p a w -> p (a w)"))
+
+        early_rows = tile("early_rows", [32, J + R], U8, tag="slot_rows")
+        deal(early_rows[:, J:], wk_s_raw[:], 2)
+        deal(late_rows[:, :R], wq_s_raw[:], 2)
+        picked_s = tile("picked_s", [P, J], U8)
+        nc.vector.tensor_copy(picked_s[:], tab_s[:].indirect(offsets[:]))
+        nc.vector.tensor_copy(early_rows[:, :J].bitcast(I32), picked_s[0:32, :].bitcast(I32))
+        spread_rows(nc.scalar, early_planes, early_rows)
+        spread_rows(nc.gpsimd, late_planes, late_rows)
+
+        wk_c = tile("wk_c", [P, PASSES, 2 * R], U8)
+        deal(wk_c[:].rearrange("p a w -> p (a w)"), wk_raw[:].rearrange("p a w -> p (a w)"), 4)
+
+        wq_raw = tile("wq_raw", [P, PASSES, R], I32, tag="slot_w")
+        nc.sync.dma_start(wq_raw[:], wq_words.rearrange("a p r i -> p a (r i)").bitcast(I32))
+
+        v_c, v_s = {}, {}
+
+        def gather(a, h):
+            lst = offsets[:, h * (BANK // 16) : (h + 1) * (BANK // 16)]
+            v_s[a, h] = early_planes[:, a, h * BANK : (h + 1) * BANK]
+            v_c[a, h] = tile("v_c%d%d" % (a, h), [P, BANK], U32)
+            nc.vector.tensor_copy(v_c[a, h][:], tab_w[a][:].bitcast(U32).indirect(lst))
+
+        def project_pass(bank, a, b, w_codes, w_scale, mov_c, mov_s, c0):
+            for t in range(PACK):
+                col = (b * PACK + t) * P
+                nc.tensor.matmul_mx(
+                    out=bank[:, t, :], lhsT=w_codes(a, col), lhsT_scale=w_scale(a, col),
+                    rhs=mov_c[:, c0 : c0 + P].bitcast(FP8X4), rhs_scale=mov_s[:, c0 : c0 + P],
+                    start=(a == 0 and t == 0), stop=(a == PASSES - 1 and t == PACK - 1))
+
+        def wk_codes(a, col):
+            return wk_c[:, a, 2 * col : 2 * (col + P)].bitcast(FP4X4)
+
+        def wk_scale(a, col):
+            return early_planes[:, a, J + col : J + col + P]
+
+        def new_bank(side, shape):
+            return psum.tile(shape, F32, name="bank" + side, tag="bank" + side)
+
+        def weave(bank, woven, blk):
+            nc.scalar.copy(woven[:, blk * P : (blk + 1) * P, :], bank[:].rearrange("p t j -> p j t"))
+
+        def quantise(woven, codes, scales):
+            nc.vector.quantize_mx(out=codes.bitcast(FP8X4), scales=scales, in_=woven[:].rearrange("p j t -> p (j t)"))
+
+        kr_c = [tile("kr_c%d%d" % (b, h), [P, BANK], U32) for b in range(PASSES) for h in range(HALVES)]
+        kr_s = [tile("kr_s%d%d" % (b, h), [P, BANK], U8) for b in range(PASSES) for h in range(HALVES)]
+
+        def finish_projection(banks, codes, scales):
+            woven = ring.tile([P, BANK, PACK], BF16, name="woven", tag="woven", align_bytes=AL, bufs=3)
+            for blk in range(PACK):
+                weave(banks[blk], woven, blk)
+            quantise(woven, codes[:], scales[:])
+
+        def load_f32(name, src, a, tag):
+            raw = tile("%s_raw%d" % (name, a), [P, PACK, BANK], F32, tag=tag)
+            nc.sync.dma_start(raw[:], src[a * 512 : (a + 1) * 512, :].rearrange("(p j) w -> p j w", j=PACK))
+            return raw
+
+        def quantise_f32(name, raw, a):
+            woven = ring.tile([P, BANK, PACK], BF16, name="cast", tag="cast", align_bytes=AL)
+            nc.vector.tensor_copy(woven[:].rearrange("p (c i) t -> p c t i", i=4),
+                                  raw[:].rearrange("p t (c i) -> p c t i", i=4))
+            codes = tile("%s_c%d" % (name, a), [P, BANK], U32)
+            scales = tile("%s_s%d" % (name, a), [P, BANK], U8)
+            quantise(woven, codes[:], scales[:])
+            return codes, scales
+
+        gather(0, 0)
+        banks = {}
+        for b in range(PASSES):
+            for blk in range(PACK):
+                banks[b, blk] = new_bank("AB"[b], [P, PACK, P])
+                project_pass(banks[b, blk], 0, b, wk_codes, wk_scale, v_c[0, 0], v_s[0, 0], blk * P)
+        gather(0, 1)
+        x_raw = [None, None]
+        x_raw[0] = load_f32("x", x, 0, "slot_tw0")
+        gather(1, 0)
+        gather(1, 1)
+        x_raw[1] = load_f32("x", x, 1, "slot_rows")
+        wvd_raw = [None, None]
+        wvd_raw[0] = load_f32("wvd", wvd, 0, "slot_tw1")
+        wq_c = tile("wq_c", [P, PASSES, R], U32)
+        for a in range(PASSES):
+            deal(wq_c[:, a, :], wq_raw[:, a, :], 8)
+        wvd_raw[1] = load_f32("wvd", wvd, 1, "slot_w")
+        for b in range(PASSES):
+            for blk in range(PACK):
+                project_pass(banks[b, blk], 1, b, wk_codes, wk_scale, v_c[1, 0], v_s[1, 0], blk * P)
+            finish_projection([banks[b, blk] for blk in range(PACK)], kr_c[2 * b], kr_s[2 * b])
+        x_q = []
+        for b in range(PASSES):
+            row = []
+            for blk in range(PACK):
+                bank = new_bank("AB"[b], [P, PACK, P])
+                for a in range(PASSES):
+                    project_pass(bank, a, b, wk_codes, wk_scale, v_c[a, 1], v_s[a, 1], blk * P)
+                row.append(bank)
+            x_q.append(quantise_f32("x", x_raw[b], b))
+            finish_projection(row, kr_c[2 * b + 1], kr_s[2 * b + 1])
+
+        def values_base(h, side):
+            row = []
+            for nt in range(N // P):
+                bank = new_bank(side, [P, BANK])
+                for a in range(PASSES):
+                    nc.tensor.matmul_mx(
+                        out=bank[:], lhsT=wv4_c[:, a, 2 * nt * P : 2 * (nt + 1) * P].bitcast(FP4X4),
+                        lhsT_scale=late_planes[:, a, R + nt * P : R + (nt + 1) * P],
+                        rhs=v_c[a, h][:].bitcast(FP8X4), rhs_scale=v_s[a, h], start=(a == 0), stop=False)
+                row.append(bank)
+            return row
+
+        def values_delta(bank, nt, h):
+            for a in range(PASSES):
+                codes, scales = wvd_q[a]
+                nc.tensor.matmul_mx(
+                    out=bank[:], lhsT=codes[:, nt * P : (nt + 1) * P].bitcast(FP8X4),
+                    lhsT_scale=scales[:, nt * P : (nt + 1) * P],
+                    rhs=v_c[a, h][:].bitcast(FP8X4), rhs_scale=v_s[a, h], start=False, stop=(a == PASSES - 1))
+            res = outs.tile([P, BANK], F32, name="res")
+            nc.scalar.copy(res[:], bank[:])
+            nc.sync.dma_start(out_1[nt * P : (nt + 1) * P, h * BANK : (h + 1) * BANK], res[:])
+
+        v_banks = values_base(0, "A")
+
+        def wq_codes(a, col):
+            return wq_c[:, a, col : col + P].bitcast(FP8X4)
+
+        def wq_scale(a, col):
+            return late_planes[:, a, col : col + P]
+
+        wvd_q = []
+        qr_q = []
+        for b in range(PASSES):
+            row = []
+            for blk in range(PACK):
+                bank = new_bank("B", [P, PACK, P])
+                for a in range(PASSES):
+                    project_pass(bank, a, b, wq_codes, wq_scale, x_q[a][0], x_q[a][1], blk * P)
+                row.append(bank)
+            wvd_q.append(quantise_f32("wvd", wvd_raw[b], b))
+            codes = tile("qr_c%d" % b, [P, M], U32)
+            scales = tile("qr_s%d" % b, [P, M], U8)
+            finish_projection(row, codes, scales)
+            qr_q.append((codes, scales))
+
+        for nt in range(N // P):
+            values_delta(v_banks[nt], nt, 0)
+
+        for h in range(HALVES):
+            for mt in range(M // P):
+                bank = new_bank("BA"[h], [P, BANK])
+                for b in range(PASSES):
+                    nc.tensor.matmul_mx(
+                        out=bank[:], lhsT=qr_q[b][0][:, mt * P : (mt + 1) * P].bitcast(FP8X4),
+                        lhsT_scale=qr_q[b][1][:, mt * P : (mt + 1) * P],
+                        rhs=kr_c[2 * b + h][:].bitcast(FP8X4), rhs_scale=kr_s[2 * b + h][:],
+                        start=(b == 0), stop=(b == PASSES - 1))
+                res = outs.tile([P, BANK], F32, name="res")
+                nc.vector.tensor_scalar(res[:], bank[:], SCORE_SCALE, None, MULT)
+                nc.sync.dma_start(out_0[mt * P : (mt + 1) * P, h * BANK : (h + 1) * BANK], res[:])
+
+        for nt in range(N // P):
+            bank = new_bank("B", [P, BANK])
+            for a in range(PASSES):
+                nc.tensor.matmul_mx(
+                    out=bank[:], lhsT=wv4_c[:, a, 2 * nt * P : 2 * (nt + 1) * P].bitcast(FP4X4),
+                    lhsT_scale=late_planes[:, a, R + nt * P : R + (nt + 1) * P],
+                    rhs=v_c[a, 1][:].bitcast(FP8X4), rhs_scale=v_s[a, 1], start=(a == 0), stop=False)
+            values_delta(bank, nt, 1)

@@ -14,6 +14,8 @@ U8 = mybir.dt.uint8
 FP8X4 = mybir.dt.float8_e4m3fn_x4
 FP4X4 = mybir.dt.float4_e2m1fn_x4
 MULT = mybir.AluOpType.mult
+ADD = mybir.AluOpType.add
+COPY = mybir.ActivationFunctionType.Copy
 
 P = 128
 PACK = 4
@@ -23,6 +25,7 @@ HALVES = J // BANK
 QUADS = 4
 SCORE_SCALE = 0.03125
 AL = 64
+KB = 1024
 
 
 def tile_list_kvt_dl_scale_kernel(tc, tab_words, tab_scales, x, wq_words, wq_scales, wk_words, wk_scales,
@@ -31,14 +34,16 @@ def tile_list_kvt_dl_scale_kernel(tc, tab_words, tab_scales, x, wq_words, wq_sca
     with ExitStack() as ctx:
         held = ctx.enter_context(tc.tile_pool(name="held", bufs=1))
         keep = ctx.enter_context(tc.tile_pool(name="keep", bufs=1))
+        placed = ctx.enter_context(tc.tile_pool(name="placed", bufs=1))
         ring = ctx.enter_context(tc.tile_pool(name="ring", bufs=2))
-        outs = ctx.enter_context(tc.tile_pool(name="outs", bufs=6))
-        psum = ctx.enter_context(tc.psum_pool(name="psum", bufs=4))
+        outs = ctx.enter_context(tc.tile_pool(name="outs", bufs=17))
+        psum = ctx.enter_context(tc.psum_pool(name="psum", bufs=8))
 
         offsets = held.tile([P, J // 16], U16, name="offsets")
-        nc.sync.dma_start(offsets[:], offs)
 
-        def tile(name, shape, dtype, tag=None):
+        def tile(name, shape, dtype, tag=None, offset=None):
+            if offset is not None:
+                return placed.tile(shape, dtype, name=name, tag=name, align_bytes=AL, offset=offset)
             return keep.tile(shape, dtype, name=name, tag=tag or name, align_bytes=AL)
 
         def zero(engine, t):
@@ -47,209 +52,214 @@ def tile_list_kvt_dl_scale_kernel(tc, tab_words, tab_scales, x, wq_words, wq_sca
         def load_rows(dst, src):
             nc.sync.dma_start(dst.bitcast(I32), src.rearrange("a q w -> q a w").bitcast(I32))
 
-        def spread_rows(queue, planes, staged):
+        def spread_rows(planes, staged):
             for q in range(QUADS):
-                queue.dma_start(planes[32 * q : 32 * q + 4].bitcast(I32), staged[8 * q : 8 * q + 8, :].bitcast(I32))
+                nc.sync.dma_start(planes[32 * q : 32 * q + 4].bitcast(I32),
+                                    staged[8 * q : 8 * q + 8, :].bitcast(I32))
 
         def deal(dst, src, run):
             nc.vector.tensor_copy(
                 dst.bitcast(I32).rearrange("p (b t g w) -> p b t g w", t=PACK, g=16, w=run),
                 src.bitcast(I32).rearrange("p (b g t w) -> p b t g w", t=PACK, g=16, w=run))
 
+        def load_f32(name, src, a, tag=None, offset=None):
+            raw = tile("%s_raw%d" % (name, a), [P, PACK, BANK], F32, tag=tag, offset=offset)
+            nc.sync.dma_start(raw[:], src[a * 512 : (a + 1) * 512, :].rearrange("(p j) w -> p j w", j=PACK))
+            return raw
+
+        def load_table(a, tag=None, offset=None):
+            words = tile("tab_w%d" % a, [P, T], I32, tag=tag, offset=offset)
+            nc.sync.dma_start(words[:], tab_words[a].rearrange("p t i -> p (t i)").bitcast(I32))
+            return words
+
+        def new_bank(shape):
+            return psum.tile(shape, F32, name="bank")
+
+        def quantise(name, woven, offset=None):
+            codes = tile(name + "_c", [P, BANK], U32, offset=offset)
+            scales = tile(name + "_s", [P, BANK], U8)
+            nc.vector.quantize_mx(out=codes[:].bitcast(FP8X4), scales=scales[:],
+                                  in_=woven[:].rearrange("p j t -> p (j t)"))
+            return codes, scales
+
+        def weave_and_quantise(name, rows, woven=None):
+            if woven is None:
+                woven = ring.tile([P, BANK, PACK], BF16, name="woven", align_bytes=AL)
+            nc.vector.tensor_copy(woven[:].rearrange("p (c i) t -> p c t i", i=4),
+                                  rows[:].rearrange("p t (c i) -> p c t i", i=4))
+            return quantise(name, woven)
+
+        def load_words(name, src, offset=None):
+            words = tile(name, [P] + list(src.shape[1:]), I32, offset=offset)
+            nc.sync.dma_start(words[:], src)
+            return words
+
         tab_s = tile("tab_s", [P, T], U8)
         load_rows(tab_s[0:32, :], tab_scales)
+        nc.sync.dma_start(offsets[:], offs)
         wk_s_raw = tile("wk_s_raw", [32, R], U8)
         load_rows(wk_s_raw[:], wk_scales)
-        wq_s_raw = tile("wq_s_raw", [32, R], U8)
-        load_rows(wq_s_raw[:], wq_scales)
-        late_rows = tile("late_rows", [32, R + N], U8)
-        load_rows(late_rows[:, R:], wv4_scales)
-        wk_raw = tile("wk_raw", [P, PASSES, 2 * R], U8, tag="slot_w")
-        nc.sync.dma_start(wk_raw[:].bitcast(I32), wk_words.rearrange("a p w -> p a w").bitcast(I32))
-        tab_w = []
-        for a in range(PASSES):
-            t = tile("tab_w%d" % a, [P, T], I32, tag="slot_tw%d" % a)
-            nc.sync.dma_start(t[:], tab_words[a].rearrange("p t i -> p (t i)").bitcast(I32))
-            tab_w.append(t)
-        wv4_c = tile("wv4_c", [P, PASSES, 2 * N], U8)
-        nc.sync.dma_start(wv4_c[:].bitcast(I32), wv4_words.rearrange("a p w -> p a w").bitcast(I32))
+        late_raw = tile("late_raw", [32, R + N], U8, offset=20 * KB)
+        load_rows(late_raw[:, :R], wq_scales)
+        load_rows(late_raw[:, R:], wv4_scales)
+        wk_raw = load_words("wk_raw", wk_words.rearrange("a p w -> p a w").bitcast(I32), 60 * KB)
+        tab_w = [load_table(0, offset=32 * KB)]
 
         zero(nc.vector, tab_s[32:64, :])
-        zero(nc.vector, tab_s[64:128, :])
-        early_planes = tile("early_planes", [P, PASSES, J + R], U8)
-        zero(nc.vector, early_planes[:].rearrange("p a w -> p (a w)"))
+        zero(nc.gpsimd, tab_s[64:128, :])
+        planes = tile("planes", [P, PASSES, J + R], U8)
+        zero(nc.vector, planes[:].rearrange("p a w -> p (a w)"))
         late_planes = tile("late_planes", [P, PASSES, R + N], U8)
         zero(nc.gpsimd, late_planes[:].rearrange("p a w -> p (a w)"))
 
-        early_rows = tile("early_rows", [32, J + R], U8, tag="slot_rows")
-        deal(early_rows[:, J:], wk_s_raw[:], 2)
-        deal(late_rows[:, :R], wq_s_raw[:], 2)
-        picked_s = tile("picked_s", [P, J], U8)
+        rows = tile("rows", [32, J + R], U8)
+        deal(rows[:, J:], wk_s_raw[:], 2)
+        picked_s = tile("picked_s", [P, J], U8, offset=16 * KB - 512)
         nc.vector.tensor_copy(picked_s[:], tab_s[:].indirect(offsets[:]))
-        nc.vector.tensor_copy(early_rows[:, :J].bitcast(I32), picked_s[0:32, :].bitcast(I32))
-        spread_rows(nc.scalar, early_planes, early_rows)
-        spread_rows(nc.gpsimd, late_planes, late_rows)
-
-        wk_c = tile("wk_c", [P, PASSES, 2 * R], U8)
+        nc.vector.tensor_copy(rows[:, :J].bitcast(I32), picked_s[0:32, :].bitcast(I32))
+        spread_rows(planes, rows)
+        tab_w.append(load_table(1, offset=0))
+        late_rows = tile("late_rows", [32, R + N], U8, offset=16 * KB)
+        deal(late_rows[:, :R], late_raw[:, :R], 2)
+        nc.vector.tensor_copy(late_rows[:, R:].bitcast(I32), late_raw[:, R:].bitcast(I32))
+        spread_rows(late_planes, late_rows)
+        wk_c = tile("wk_c", [P, PASSES, 2 * R], U8, offset=20 * KB)
         deal(wk_c[:].rearrange("p a w -> p (a w)"), wk_raw[:].rearrange("p a w -> p (a w)"), 4)
-
-        wq_raw = tile("wq_raw", [P, PASSES, R], I32, tag="slot_w")
-        nc.sync.dma_start(wq_raw[:], wq_words.rearrange("a p r i -> p a (r i)").bitcast(I32))
+        wv4_c = tile("wv4_c", [P, PASSES, 2 * N], U8, offset=60 * KB)
+        nc.sync.dma_start(wv4_c[:].bitcast(I32), wv4_words.rearrange("a p w -> p a w").bitcast(I32))
+        wvd_raw = [load_f32("wvd", wvd, 0, offset=62 * KB)]
 
         v_c, v_s = {}, {}
 
         def gather(a, h):
             lst = offsets[:, h * (BANK // 16) : (h + 1) * (BANK // 16)]
-            v_s[a, h] = early_planes[:, a, h * BANK : (h + 1) * BANK]
+            v_s[a, h] = planes[:, a, h * BANK : (h + 1) * BANK]
             v_c[a, h] = tile("v_c%d%d" % (a, h), [P, BANK], U32)
             nc.vector.tensor_copy(v_c[a, h][:], tab_w[a][:].bitcast(U32).indirect(lst))
 
-        def project_pass(bank, a, b, w_codes, w_scale, mov_c, mov_s, c0):
+        def key_pass(out, a, b, t, h, cols, start, stop):
+            col = (b * PACK + t) * P
+            nc.tensor.matmul_mx(
+                out=out, lhsT=wk_c[:, a, 2 * col : 2 * (col + P)].bitcast(FP4X4),
+                lhsT_scale=planes[:, a, J + col : J + col + P],
+                rhs=v_c[a, h][:, cols].bitcast(FP8X4), rhs_scale=v_s[a, h][:, cols], start=start, stop=stop)
+
+        k_banks = {}
+
+        def narrow_key_passes(a, b, blk):
             for t in range(PACK):
-                col = (b * PACK + t) * P
-                nc.tensor.matmul_mx(
-                    out=bank[:, t, :], lhsT=w_codes(a, col), lhsT_scale=w_scale(a, col),
-                    rhs=mov_c[:, c0 : c0 + P].bitcast(FP8X4), rhs_scale=mov_s[:, c0 : c0 + P],
-                    start=(a == 0 and t == 0), stop=(a == PASSES - 1 and t == PACK - 1))
-
-        def wk_codes(a, col):
-            return wk_c[:, a, 2 * col : 2 * (col + P)].bitcast(FP4X4)
-
-        def wk_scale(a, col):
-            return early_planes[:, a, J + col : J + col + P]
-
-        def new_bank(side, shape):
-            return psum.tile(shape, F32, name="bank" + side, tag="bank" + side)
-
-        def weave(bank, woven, blk):
-            nc.scalar.copy(woven[:, blk * P : (blk + 1) * P, :], bank[:].rearrange("p t j -> p j t"))
-
-        def quantise(woven, codes, scales):
-            nc.vector.quantize_mx(out=codes.bitcast(FP8X4), scales=scales, in_=woven[:].rearrange("p j t -> p (j t)"))
-
-        kr_c = [tile("kr_c%d%d" % (b, h), [P, BANK], U32) for b in range(PASSES) for h in range(HALVES)]
-        kr_s = [tile("kr_s%d%d" % (b, h), [P, BANK], U8) for b in range(PASSES) for h in range(HALVES)]
-
-        def finish_projection(banks, codes, scales):
-            woven = ring.tile([P, BANK, PACK], BF16, name="woven", tag="woven", align_bytes=AL, bufs=3)
-            for blk in range(PACK):
-                weave(banks[blk], woven, blk)
-            quantise(woven, codes[:], scales[:])
-
-        def load_f32(name, src, a, tag):
-            raw = tile("%s_raw%d" % (name, a), [P, PACK, BANK], F32, tag=tag)
-            nc.sync.dma_start(raw[:], src[a * 512 : (a + 1) * 512, :].rearrange("(p j) w -> p j w", j=PACK))
-            return raw
-
-        def quantise_f32(name, raw, a):
-            woven = ring.tile([P, BANK, PACK], BF16, name="cast", tag="cast", align_bytes=AL)
-            nc.vector.tensor_copy(woven[:].rearrange("p (c i) t -> p c t i", i=4),
-                                  raw[:].rearrange("p t (c i) -> p c t i", i=4))
-            codes = tile("%s_c%d" % (name, a), [P, BANK], U32)
-            scales = tile("%s_s%d" % (name, a), [P, BANK], U8)
-            quantise(woven, codes[:], scales[:])
-            return codes, scales
+                key_pass(k_banks[b, blk][:, t, :], a, b, t, 0, slice(blk * P, (blk + 1) * P),
+                         a == 0 and t == 0, a == PASSES - 1 and t == PACK - 1)
 
         gather(0, 0)
-        banks = {}
-        for b in range(PASSES):
-            for blk in range(PACK):
-                banks[b, blk] = new_bank("AB"[b], [P, PACK, P])
-                project_pass(banks[b, blk], 0, b, wk_codes, wk_scale, v_c[0, 0], v_s[0, 0], blk * P)
         gather(0, 1)
-        x_raw = [None, None]
-        x_raw[0] = load_f32("x", x, 0, "slot_tw0")
+        wvd_raw.append(load_f32("wvd", wvd, 1, offset=26 * KB))
+        wq_rows = [wq_words[a].rearrange("p r i -> p (r i)").bitcast(I32) for a in range(PASSES)]
+        wq_raw = [load_words("wq_raw0", wq_rows[0], 34 * KB)]
+        x_raw = [load_f32("x", x, 0, offset=42 * KB)]
+        wq_raw.append(load_words("wq_raw1", wq_rows[1], 38 * KB))
+        for b in range(PASSES):
+            for blk in range(BANK // P):
+                k_banks[b, blk] = new_bank([P, PACK, P])
+                narrow_key_passes(0, b, blk)
         gather(1, 0)
         gather(1, 1)
-        x_raw[1] = load_f32("x", x, 1, "slot_rows")
-        wvd_raw = [None, None]
-        wvd_raw[0] = load_f32("wvd", wvd, 0, "slot_tw1")
-        wq_c = tile("wq_c", [P, PASSES, R], U32)
+        x_raw.append(load_f32("x", x, 1, offset=8 * KB))
+        k_woven = []
+        for b in range(PASSES):
+            k_woven.append(tile("k_woven%d" % b, [P, BANK, PACK], BF16))
+            for blk in range(BANK // P):
+                narrow_key_passes(1, b, blk)
+                nc.scalar.copy(k_woven[b][:, blk * P : (blk + 1) * P, :], k_banks[b, blk][:].rearrange("p t j -> p j t"))
+        k_rows = []
+        for b in range(PASSES):
+            k_rows.append(tile("k_rows%d" % b, [P, PACK, BANK], BF16))
+            for t in range(PACK):
+                bank = new_bank([P, BANK])
+                for a in range(PASSES):
+                    key_pass(bank[:], a, b, t, 1, slice(0, BANK), a == 0, a == PASSES - 1)
+                nc.scalar.copy(k_rows[b][:, t, :], bank[:])
+
+        wvd_q, kr_q = {}, {}
+        wvd_woven = tile("wvd_woven", [P, PASSES, N, PACK], BF16, offset=0)
         for a in range(PASSES):
-            deal(wq_c[:, a, :], wq_raw[:, a, :], 8)
-        wvd_raw[1] = load_f32("wvd", wvd, 1, "slot_w")
+            wvd_q[a] = weave_and_quantise("wvd%d" % a, wvd_raw[a], wvd_woven[:, a])
         for b in range(PASSES):
-            for blk in range(PACK):
-                project_pass(banks[b, blk], 1, b, wk_codes, wk_scale, v_c[1, 0], v_s[1, 0], blk * P)
-            finish_projection([banks[b, blk] for blk in range(PACK)], kr_c[2 * b], kr_s[2 * b])
-        x_q = []
-        for b in range(PASSES):
-            row = []
-            for blk in range(PACK):
-                bank = new_bank("AB"[b], [P, PACK, P])
-                for a in range(PASSES):
-                    project_pass(bank, a, b, wk_codes, wk_scale, v_c[a, 1], v_s[a, 1], blk * P)
-                row.append(bank)
-            x_q.append(quantise_f32("x", x_raw[b], b))
-            finish_projection(row, kr_c[2 * b + 1], kr_s[2 * b + 1])
+            kr_q[b, 0] = quantise("kr%d0" % b, k_woven[b], (62 * KB, 26 * KB)[b])
 
-        def values_base(h, side):
-            row = []
-            for nt in range(N // P):
-                bank = new_bank(side, [P, BANK])
-                for a in range(PASSES):
-                    nc.tensor.matmul_mx(
-                        out=bank[:], lhsT=wv4_c[:, a, 2 * nt * P : 2 * (nt + 1) * P].bitcast(FP4X4),
-                        lhsT_scale=late_planes[:, a, R + nt * P : R + (nt + 1) * P],
-                        rhs=v_c[a, h][:].bitcast(FP8X4), rhs_scale=v_s[a, h], start=(a == 0), stop=False)
-                row.append(bank)
-            return row
-
-        def values_delta(bank, nt, h):
-            for a in range(PASSES):
-                codes, scales = wvd_q[a]
-                nc.tensor.matmul_mx(
-                    out=bank[:], lhsT=codes[:, nt * P : (nt + 1) * P].bitcast(FP8X4),
-                    lhsT_scale=scales[:, nt * P : (nt + 1) * P],
-                    rhs=v_c[a, h][:].bitcast(FP8X4), rhs_scale=v_s[a, h], start=False, stop=(a == PASSES - 1))
-            res = outs.tile([P, BANK], F32, name="res")
-            nc.scalar.copy(res[:], bank[:])
-            nc.sync.dma_start(out_1[nt * P : (nt + 1) * P, h * BANK : (h + 1) * BANK], res[:])
-
-        v_banks = values_base(0, "A")
-
-        def wq_codes(a, col):
-            return wq_c[:, a, col : col + P].bitcast(FP8X4)
-
-        def wq_scale(a, col):
-            return late_planes[:, a, col : col + P]
-
-        wvd_q = []
-        qr_q = []
-        for b in range(PASSES):
-            row = []
-            for blk in range(PACK):
-                bank = new_bank("B", [P, PACK, P])
-                for a in range(PASSES):
-                    project_pass(bank, a, b, wq_codes, wq_scale, x_q[a][0], x_q[a][1], blk * P)
-                row.append(bank)
-            wvd_q.append(quantise_f32("wvd", wvd_raw[b], b))
-            codes = tile("qr_c%d" % b, [P, M], U32)
-            scales = tile("qr_s%d" % b, [P, M], U8)
-            finish_projection(row, codes, scales)
-            qr_q.append((codes, scales))
-
-        for nt in range(N // P):
-            values_delta(v_banks[nt], nt, 0)
-
-        for h in range(HALVES):
-            for mt in range(M // P):
-                bank = new_bank("BA"[h], [P, BANK])
-                for b in range(PASSES):
-                    nc.tensor.matmul_mx(
-                        out=bank[:], lhsT=qr_q[b][0][:, mt * P : (mt + 1) * P].bitcast(FP8X4),
-                        lhsT_scale=qr_q[b][1][:, mt * P : (mt + 1) * P],
-                        rhs=kr_c[2 * b + h][:].bitcast(FP8X4), rhs_scale=kr_s[2 * b + h][:],
-                        start=(b == 0), stop=(b == PASSES - 1))
-                res = outs.tile([P, BANK], F32, name="res")
-                nc.vector.tensor_scalar(res[:], bank[:], SCORE_SCALE, None, MULT)
-                nc.sync.dma_start(out_0[mt * P : (mt + 1) * P, h * BANK : (h + 1) * BANK], res[:])
-
-        for nt in range(N // P):
-            bank = new_bank("B", [P, BANK])
+        def values(nt, h, on_vector):
+            bank = new_bank([P, BANK])
+            cols = slice(nt * P, (nt + 1) * P)
             for a in range(PASSES):
                 nc.tensor.matmul_mx(
                     out=bank[:], lhsT=wv4_c[:, a, 2 * nt * P : 2 * (nt + 1) * P].bitcast(FP4X4),
                     lhsT_scale=late_planes[:, a, R + nt * P : R + (nt + 1) * P],
-                    rhs=v_c[a, 1][:].bitcast(FP8X4), rhs_scale=v_s[a, 1], start=(a == 0), stop=False)
-            values_delta(bank, nt, 1)
+                    rhs=v_c[a, h][:].bitcast(FP8X4), rhs_scale=v_s[a, h], start=(a == 0), stop=False)
+            for a in range(PASSES):
+                nc.tensor.matmul_mx(
+                    out=bank[:], lhsT=wvd_q[a][0][:, cols].bitcast(FP8X4), lhsT_scale=wvd_q[a][1][:, cols],
+                    rhs=v_c[a, h][:].bitcast(FP8X4), rhs_scale=v_s[a, h], start=False, stop=(a == PASSES - 1))
+            res = outs.tile([P, BANK], F32, name="res")
+            if on_vector:
+                nc.vector.tensor_copy(res[:], bank[:])
+            else:
+                nc.scalar.copy(res[:], bank[:])
+            nc.sync.dma_start(out_1[cols, h * BANK : (h + 1) * BANK], res[:])
+
+        for nt in range(N // P):
+            values(nt, 0, False)
+
+        wq_c, x_q = [], []
+        for a in range(PASSES):
+            wq_c.append(tile("wq_c%d" % a, [P, R], U32, offset=(0, 34 * KB)[a]))
+            deal(wq_c[a][:], wq_raw[a][:], 8)
+            woven = tile("x_woven0", [P, M, PACK], BF16, offset=4 * KB) if a == 0 else None
+            x_q.append(weave_and_quantise("x%d" % a, x_raw[a], woven))
+        for b in range(PASSES):
+            kr_q[b, 1] = weave_and_quantise("kr%d1" % b, k_rows[b])
+
+        def query_passes(bank, a, b, blk):
+            cols = slice(blk * P, (blk + 1) * P)
+            for t in range(PACK):
+                col = (b * PACK + t) * P
+                nc.tensor.matmul_mx(
+                    out=bank[:, t, :], lhsT=wq_c[a][:, col : col + P].bitcast(FP8X4),
+                    lhsT_scale=late_planes[:, a, col : col + P],
+                    rhs=x_q[a][0][:, cols].bitcast(FP8X4), rhs_scale=x_q[a][1][:, cols],
+                    start=(a == 0 and t == 0), stop=(a == PASSES - 1 and t == PACK - 1))
+
+        qr_q = []
+        for b in range(PASSES):
+            q_woven = tile("q_woven%d" % b, [P, M, PACK], BF16)
+            q_banks = [new_bank([P, PACK, P]) for blk in range(M // P)]
+            for blk in range(M // P):
+                query_passes(q_banks[blk], 0, b, blk)
+            for blk in range(M // P):
+                query_passes(q_banks[blk], 1, b, blk)
+                nc.scalar.copy(q_woven[:, blk * P : (blk + 1) * P, :], q_banks[blk][:].rearrange("p t j -> p j t"))
+            qr_q.append(quantise("qr%d" % b, q_woven))
+
+        for nt in range(N // P):
+            values(nt, 1, True)
+
+        def scores(mt, h, c0, width, on_vector):
+            bank = new_bank([P, width])
+            m_cols = slice(mt * P, (mt + 1) * P)
+            cols = slice(c0, c0 + width)
+            for b in range(PASSES):
+                nc.tensor.matmul_mx(
+                    out=bank[:], lhsT=qr_q[b][0][:, m_cols].bitcast(FP8X4), lhsT_scale=qr_q[b][1][:, m_cols],
+                    rhs=kr_q[b, h][0][:, cols].bitcast(FP8X4), rhs_scale=kr_q[b, h][1][:, cols],
+                    start=(b == 0), stop=(b == PASSES - 1))
+            res = outs.tile([P, width], F32, name="res")
+            if on_vector:
+                nc.vector.tensor_scalar(res[:], bank[:], SCORE_SCALE, None, MULT)
+            else:
+                nc.scalar.activation(res[:], bank[:], COPY, scale=SCORE_SCALE)
+            nc.sync.dma_start(out_0[m_cols, h * BANK + c0 : h * BANK + c0 + width], res[:])
+
+        score_tiles = [(mt, h) for mt in range(M // P) for h in range(HALVES)]
+        for i, (mt, h) in enumerate(score_tiles[:-1]):
+            scores(mt, h, 0, BANK, i % 2 == 1)
+        for half in range(2):
+            scores(*score_tiles[-1], half * BANK // 2, BANK // 2, half == 0)

@@ -14,96 +14,128 @@ U8 = mybir.dt.uint8
 FP8X4 = mybir.dt.float8_e4m3fn_x4
 FP4X4 = mybir.dt.float4_e2m1fn_x4
 MULT = mybir.AluOpType.mult
-ADD = mybir.AluOpType.add
 COPY = mybir.ActivationFunctionType.Copy
 
 P = 128
 PACK = 4
 PASSES = 2
+K_PASS = P * PACK
 BANK = 512
 HALVES = J // BANK
 QUADS = 4
+BLOCKS = 16
+SCALE_ROWS = PASSES * BLOCKS
+LIST_ROWS = 16
+LINE = 4
 SCORE_SCALE = 0.03125
-AL = 64
+ALIGN = 64
+PSUM_BANKS = 8
+RESULT_TILES = 17
+EARLY_VALUE_TILES = 5
+
 KB = 1024
+AT_TABLE = (32 * KB, 0)
+AT_PICKED_SCALES = 16 * KB - 512
+AT_LATE_ROWS = 16 * KB
+AT_LATE_RAW = 20 * KB
+AT_WK_CODES = 20 * KB
+AT_WK_RAW = 60 * KB
+AT_WV4_CODES = 60 * KB
+AT_WVD_RAW = (62 * KB, 26 * KB)
+AT_WQ_RAW = (34 * KB, 8 * KB)
+AT_X_RAW = (42 * KB, 12 * KB)
+AT_WVD_WOVEN = 0
+AT_KR_CODES = AT_WVD_RAW
+AT_X_WOVEN = (4 * KB, 38 * KB)
+AT_WQ_CODES = (0, 38 * KB)
+AT_KR_ROWS = (70 * KB, None)
+AT_KR_WOVEN = (8 * KB, 70 * KB)
 
 
-def tile_list_kvt_dl_scale_kernel(tc, tab_words, tab_scales, x, wq_words, wq_scales, wk_words, wk_scales,
-        wv4_words, wv4_scales, wvd, offs, out_0, out_1):
+def tile_list_kvt_dl_scale_kernel(
+    tc, tab_words, tab_scales, x, wq_words, wq_scales, wk_words, wk_scales, wv4_words, wv4_scales, wvd, offs,
+    out_0, out_1,
+):
     nc = tc.nc
     with ExitStack() as ctx:
         held = ctx.enter_context(tc.tile_pool(name="held", bufs=1))
         keep = ctx.enter_context(tc.tile_pool(name="keep", bufs=1))
         placed = ctx.enter_context(tc.tile_pool(name="placed", bufs=1))
-        ring = ctx.enter_context(tc.tile_pool(name="ring", bufs=2))
-        outs = ctx.enter_context(tc.tile_pool(name="outs", bufs=17))
-        psum = ctx.enter_context(tc.psum_pool(name="psum", bufs=8))
+        outs = ctx.enter_context(tc.tile_pool(name="outs", bufs=RESULT_TILES))
+        psum = ctx.enter_context(tc.psum_pool(name="psum", bufs=PSUM_BANKS))
 
-        offsets = held.tile([P, J // 16], U16, name="offsets")
+        offsets = held.tile([P, J // LIST_ROWS], U16, name="offsets")
 
-        def tile(name, shape, dtype, tag=None, offset=None):
-            if offset is not None:
-                return placed.tile(shape, dtype, name=name, tag=name, align_bytes=AL, offset=offset)
-            return keep.tile(shape, dtype, name=name, tag=tag or name, align_bytes=AL)
-
-        def zero(engine, t):
-            engine.memset(t.bitcast(I32), 0)
-
-        def load_rows(dst, src):
-            nc.sync.dma_start(dst.bitcast(I32), src.rearrange("a q w -> q a w").bitcast(I32))
-
-        def spread_rows(planes, staged):
-            for q in range(QUADS):
-                nc.sync.dma_start(planes[32 * q : 32 * q + 4].bitcast(I32),
-                                    staged[8 * q : 8 * q + 8, :].bitcast(I32))
-
-        def deal(dst, src, run):
-            nc.vector.tensor_copy(
-                dst.bitcast(I32).rearrange("p (b t g w) -> p b t g w", t=PACK, g=16, w=run),
-                src.bitcast(I32).rearrange("p (b g t w) -> p b t g w", t=PACK, g=16, w=run))
-
-        def load_f32(name, src, a, tag=None, offset=None):
-            raw = tile("%s_raw%d" % (name, a), [P, PACK, BANK], F32, tag=tag, offset=offset)
-            nc.sync.dma_start(raw[:], src[a * 512 : (a + 1) * 512, :].rearrange("(p j) w -> p j w", j=PACK))
-            return raw
-
-        def load_table(a, tag=None, offset=None):
-            words = tile("tab_w%d" % a, [P, T], I32, tag=tag, offset=offset)
-            nc.sync.dma_start(words[:], tab_words[a].rearrange("p t i -> p (t i)").bitcast(I32))
-            return words
+        def tile(name, shape, dtype, offset=None):
+            if offset is None:
+                return keep.tile(shape, dtype, name=name, tag=name, align_bytes=ALIGN)
+            return placed.tile(shape, dtype, name=name, tag=name, align_bytes=ALIGN, offset=offset)
 
         def new_bank(shape):
             return psum.tile(shape, F32, name="bank")
 
-        def quantise(name, woven, offset=None):
-            codes = tile(name + "_c", [P, BANK], U32, offset=offset)
-            scales = tile(name + "_s", [P, BANK], U8)
-            nc.vector.quantize_mx(out=codes[:].bitcast(FP8X4), scales=scales[:],
-                                  in_=woven[:].rearrange("p j t -> p (j t)"))
-            return codes, scales
+        def zero(engine, region):
+            engine.memset(region.bitcast(I32), 0)
 
-        def weave_and_quantise(name, rows, woven=None):
-            if woven is None:
-                woven = ring.tile([P, BANK, PACK], BF16, name="woven", align_bytes=AL)
-            nc.vector.tensor_copy(woven[:].rearrange("p (c i) t -> p c t i", i=4),
-                                  rows[:].rearrange("p t (c i) -> p c t i", i=4))
-            return quantise(name, woven)
+        def load_scale_rows(dst, src):
+            nc.sync.dma_start(dst.bitcast(I32), src.rearrange("a g w -> g a w").bitcast(I32))
 
-        def load_words(name, src, offset=None):
-            words = tile(name, [P] + list(src.shape[1:]), I32, offset=offset)
+        def spread_scale_rows(planes, staged):
+            for q in range(QUADS):
+                nc.sync.dma_start(
+                    planes[32 * q : 32 * q + 4].bitcast(I32), staged[8 * q : 8 * q + 8, :].bitcast(I32)
+                )
+
+        def load_words(name, src, offset):
+            words = tile(name, [P] + list(src.shape[1:]), I32, offset)
             nc.sync.dma_start(words[:], src)
             return words
 
+        def load_table(a):
+            return load_words("tab_w%d" % a, tab_words[a].rearrange("p t i -> p (t i)").bitcast(I32), AT_TABLE[a])
+
+        def load_wq(b):
+            src = wq_words[:, :, b * K_PASS : (b + 1) * K_PASS, :]
+            return load_words("wq_raw%d" % b, src.rearrange("a p r i -> p a (r i)").bitcast(I32), AT_WQ_RAW[b])
+
+        def load_f32(name, src, a, offset):
+            raw = tile("%s_raw%d" % (name, a), [P, PACK, BANK], F32, offset)
+            nc.sync.dma_start(raw[:], src[a * K_PASS : (a + 1) * K_PASS, :].rearrange("(p t) w -> p t w", t=PACK))
+            return raw
+
+        def deal(dst, src, run):
+            nc.vector.tensor_copy(
+                dst.bitcast(I32).rearrange("p (c t g w) -> p c t g w", t=PACK, g=BLOCKS, w=run),
+                src.bitcast(I32).rearrange("p (c g t w) -> p c t g w", t=PACK, g=BLOCKS, w=run),
+            )
+
+        def quantise(name, woven, offset=None):
+            codes = tile(name + "_c", [P, BANK], U32, offset)
+            scales = tile(name + "_s", [P, BANK], U8)
+            nc.vector.quantize_mx(
+                out=codes[:].bitcast(FP8X4), scales=scales[:], in_=woven[:].rearrange("p j t -> p (j t)")
+            )
+            return codes, scales
+
+        def weave_and_quantise(name, rows, woven):
+            nc.vector.tensor_copy(
+                woven[:].rearrange("p (c i) t -> p c t i", i=LINE), rows[:].rearrange("p t (c i) -> p c t i", i=LINE)
+            )
+            return quantise(name, woven)
+
+        def weave_out_of_bank(woven, blk, bank):
+            nc.scalar.copy(woven[:, blk * P : (blk + 1) * P, :], bank[:].rearrange("p t j -> p j t"))
+
         tab_s = tile("tab_s", [P, T], U8)
-        load_rows(tab_s[0:32, :], tab_scales)
+        load_scale_rows(tab_s[0:SCALE_ROWS, :], tab_scales)
         nc.sync.dma_start(offsets[:], offs)
-        wk_s_raw = tile("wk_s_raw", [32, R], U8)
-        load_rows(wk_s_raw[:], wk_scales)
-        late_raw = tile("late_raw", [32, R + N], U8, offset=20 * KB)
-        load_rows(late_raw[:, :R], wq_scales)
-        load_rows(late_raw[:, R:], wv4_scales)
-        wk_raw = load_words("wk_raw", wk_words.rearrange("a p w -> p a w").bitcast(I32), 60 * KB)
-        tab_w = [load_table(0, offset=32 * KB)]
+        wk_s_raw = tile("wk_s_raw", [SCALE_ROWS, R], U8)
+        load_scale_rows(wk_s_raw[:], wk_scales)
+        late_raw = tile("late_raw", [SCALE_ROWS, R + N], U8, AT_LATE_RAW)
+        load_scale_rows(late_raw[:, :R], wq_scales)
+        load_scale_rows(late_raw[:, R:], wv4_scales)
+        wk_raw = load_words("wk_raw", wk_words.rearrange("a p w -> p a w").bitcast(I32), AT_WK_RAW)
+        tab_w = [load_table(0)]
 
         zero(nc.vector, tab_s[32:64, :])
         zero(nc.gpsimd, tab_s[64:128, :])
@@ -112,68 +144,73 @@ def tile_list_kvt_dl_scale_kernel(tc, tab_words, tab_scales, x, wq_words, wq_sca
         late_planes = tile("late_planes", [P, PASSES, R + N], U8)
         zero(nc.gpsimd, late_planes[:].rearrange("p a w -> p (a w)"))
 
-        rows = tile("rows", [32, J + R], U8)
-        deal(rows[:, J:], wk_s_raw[:], 2)
-        picked_s = tile("picked_s", [P, J], U8, offset=16 * KB - 512)
-        nc.vector.tensor_copy(picked_s[:], tab_s[:].indirect(offsets[:]))
-        nc.vector.tensor_copy(rows[:, :J].bitcast(I32), picked_s[0:32, :].bitcast(I32))
-        spread_rows(planes, rows)
-        tab_w.append(load_table(1, offset=0))
-        late_rows = tile("late_rows", [32, R + N], U8, offset=16 * KB)
+        early_rows = tile("rows", [SCALE_ROWS, J + R], U8)
+        deal(early_rows[:, J:], wk_s_raw[:], 2)
+        picked_scales = tile("picked_s", [P, J], U8, AT_PICKED_SCALES)
+        nc.vector.tensor_copy(picked_scales[:], tab_s[:].indirect(offsets[:]))
+        nc.vector.tensor_copy(early_rows[:, :J].bitcast(I32), picked_scales[0:SCALE_ROWS, :].bitcast(I32))
+        spread_scale_rows(planes, early_rows)
+        tab_w.append(load_table(1))
+        late_rows = tile("late_rows", [SCALE_ROWS, R + N], U8, AT_LATE_ROWS)
         deal(late_rows[:, :R], late_raw[:, :R], 2)
         nc.vector.tensor_copy(late_rows[:, R:].bitcast(I32), late_raw[:, R:].bitcast(I32))
-        spread_rows(late_planes, late_rows)
-        wk_c = tile("wk_c", [P, PASSES, 2 * R], U8, offset=20 * KB)
+        spread_scale_rows(late_planes, late_rows)
+        wk_c = tile("wk_c", [P, PASSES, 2 * R], U8, AT_WK_CODES)
         deal(wk_c[:].rearrange("p a w -> p (a w)"), wk_raw[:].rearrange("p a w -> p (a w)"), 4)
-        wv4_c = tile("wv4_c", [P, PASSES, 2 * N], U8, offset=60 * KB)
+        wv4_c = tile("wv4_c", [P, PASSES, 2 * N], U8, AT_WV4_CODES)
         nc.sync.dma_start(wv4_c[:].bitcast(I32), wv4_words.rearrange("a p w -> p a w").bitcast(I32))
-        wvd_raw = [load_f32("wvd", wvd, 0, offset=62 * KB)]
+        wvd_raw = [load_f32("wvd", wvd, 0, AT_WVD_RAW[0])]
 
         v_c, v_s = {}, {}
 
         def gather(a, h):
-            lst = offsets[:, h * (BANK // 16) : (h + 1) * (BANK // 16)]
+            entries = offsets[:, h * (BANK // LIST_ROWS) : (h + 1) * (BANK // LIST_ROWS)]
             v_s[a, h] = planes[:, a, h * BANK : (h + 1) * BANK]
             v_c[a, h] = tile("v_c%d%d" % (a, h), [P, BANK], U32)
-            nc.vector.tensor_copy(v_c[a, h][:], tab_w[a][:].bitcast(U32).indirect(lst))
+            nc.vector.tensor_copy(v_c[a, h][:], tab_w[a][:].bitcast(U32).indirect(entries))
 
         def key_pass(out, a, b, t, h, cols, start, stop):
             col = (b * PACK + t) * P
             nc.tensor.matmul_mx(
-                out=out, lhsT=wk_c[:, a, 2 * col : 2 * (col + P)].bitcast(FP4X4),
+                out=out,
+                lhsT=wk_c[:, a, 2 * col : 2 * (col + P)].bitcast(FP4X4),
                 lhsT_scale=planes[:, a, J + col : J + col + P],
-                rhs=v_c[a, h][:, cols].bitcast(FP8X4), rhs_scale=v_s[a, h][:, cols], start=start, stop=stop)
+                rhs=v_c[a, h][:, cols].bitcast(FP8X4),
+                rhs_scale=v_s[a, h][:, cols],
+                start=start,
+                stop=stop,
+            )
 
         k_banks = {}
 
         def narrow_key_passes(a, b, blk):
             for t in range(PACK):
-                key_pass(k_banks[b, blk][:, t, :], a, b, t, 0, slice(blk * P, (blk + 1) * P),
-                         a == 0 and t == 0, a == PASSES - 1 and t == PACK - 1)
+                first, last = a == 0 and t == 0, a == PASSES - 1 and t == PACK - 1
+                key_pass(k_banks[b, blk][:, t, :], a, b, t, 0, slice(blk * P, (blk + 1) * P), first, last)
 
         gather(0, 0)
         gather(0, 1)
-        wvd_raw.append(load_f32("wvd", wvd, 1, offset=26 * KB))
-        wq_rows = [wq_words[a].rearrange("p r i -> p (r i)").bitcast(I32) for a in range(PASSES)]
-        wq_raw = [load_words("wq_raw0", wq_rows[0], 34 * KB)]
-        x_raw = [load_f32("x", x, 0, offset=42 * KB)]
-        wq_raw.append(load_words("wq_raw1", wq_rows[1], 38 * KB))
+        wvd_raw.append(load_f32("wvd", wvd, 1, AT_WVD_RAW[1]))
+        wq_raw = [load_wq(0)]
+        x_raw = [load_f32("x", x, 0, AT_X_RAW[0])]
         for b in range(PASSES):
             for blk in range(BANK // P):
                 k_banks[b, blk] = new_bank([P, PACK, P])
                 narrow_key_passes(0, b, blk)
         gather(1, 0)
         gather(1, 1)
-        x_raw.append(load_f32("x", x, 1, offset=8 * KB))
+        x_raw.append(load_f32("x", x, 1, AT_X_RAW[1]))
+        wq_raw.append(load_wq(1))
         k_woven = []
         for b in range(PASSES):
             k_woven.append(tile("k_woven%d" % b, [P, BANK, PACK], BF16))
             for blk in range(BANK // P):
                 narrow_key_passes(1, b, blk)
-                nc.scalar.copy(k_woven[b][:, blk * P : (blk + 1) * P, :], k_banks[b, blk][:].rearrange("p t j -> p j t"))
+                weave_out_of_bank(k_woven[b], blk, k_banks[b, blk])
+
         k_rows = []
         for b in range(PASSES):
-            k_rows.append(tile("k_rows%d" % b, [P, PACK, BANK], BF16))
+            k_rows.append(tile("k_rows%d" % b, [P, PACK, BANK], BF16, AT_KR_ROWS[b]))
             for t in range(PACK):
                 bank = new_bank([P, BANK])
                 for a in range(PASSES):
@@ -181,52 +218,74 @@ def tile_list_kvt_dl_scale_kernel(tc, tab_words, tab_scales, x, wq_words, wq_sca
                 nc.scalar.copy(k_rows[b][:, t, :], bank[:])
 
         wvd_q, kr_q = {}, {}
-        wvd_woven = tile("wvd_woven", [P, PASSES, N, PACK], BF16, offset=0)
+        wvd_woven = tile("wvd_woven", [P, PASSES, N, PACK], BF16, AT_WVD_WOVEN)
         for a in range(PASSES):
             wvd_q[a] = weave_and_quantise("wvd%d" % a, wvd_raw[a], wvd_woven[:, a])
         for b in range(PASSES):
-            kr_q[b, 0] = quantise("kr%d0" % b, k_woven[b], (62 * KB, 26 * KB)[b])
+            kr_q[b, 0] = quantise("kr%d0" % b, k_woven[b], AT_KR_CODES[b])
 
         def values(nt, h, on_vector):
             bank = new_bank([P, BANK])
-            cols = slice(nt * P, (nt + 1) * P)
+            n_cols = slice(nt * P, (nt + 1) * P)
             for a in range(PASSES):
                 nc.tensor.matmul_mx(
-                    out=bank[:], lhsT=wv4_c[:, a, 2 * nt * P : 2 * (nt + 1) * P].bitcast(FP4X4),
+                    out=bank[:],
+                    lhsT=wv4_c[:, a, 2 * nt * P : 2 * (nt + 1) * P].bitcast(FP4X4),
                     lhsT_scale=late_planes[:, a, R + nt * P : R + (nt + 1) * P],
-                    rhs=v_c[a, h][:].bitcast(FP8X4), rhs_scale=v_s[a, h], start=(a == 0), stop=False)
+                    rhs=v_c[a, h][:].bitcast(FP8X4),
+                    rhs_scale=v_s[a, h],
+                    start=(a == 0),
+                    stop=False,
+                )
             for a in range(PASSES):
                 nc.tensor.matmul_mx(
-                    out=bank[:], lhsT=wvd_q[a][0][:, cols].bitcast(FP8X4), lhsT_scale=wvd_q[a][1][:, cols],
-                    rhs=v_c[a, h][:].bitcast(FP8X4), rhs_scale=v_s[a, h], start=False, stop=(a == PASSES - 1))
+                    out=bank[:],
+                    lhsT=wvd_q[a][0][:, n_cols].bitcast(FP8X4),
+                    lhsT_scale=wvd_q[a][1][:, n_cols],
+                    rhs=v_c[a, h][:].bitcast(FP8X4),
+                    rhs_scale=v_s[a, h],
+                    start=False,
+                    stop=(a == PASSES - 1),
+                )
             res = outs.tile([P, BANK], F32, name="res")
             if on_vector:
                 nc.vector.tensor_copy(res[:], bank[:])
             else:
                 nc.scalar.copy(res[:], bank[:])
-            nc.sync.dma_start(out_1[cols, h * BANK : (h + 1) * BANK], res[:])
+            nc.sync.dma_start(out_1[n_cols, h * BANK : (h + 1) * BANK], res[:])
 
-        for nt in range(N // P):
-            values(nt, 0, False)
+        value_tiles = [(nt, h) for h in range(HALVES) for nt in range(N // P)]
+        for nt, h in value_tiles[:EARLY_VALUE_TILES]:
+            values(nt, h, False)
 
-        wq_c, x_q = [], []
+        def deal_wq(b):
+            codes = tile("wq_c%d" % b, [P, PASSES, K_PASS], U32, AT_WQ_CODES[b])
+            deal(codes[:].rearrange("p a r -> p (a r)"), wq_raw[b][:].rearrange("p a r -> p (a r)"), 8)
+            return codes
+
+        wq_c = [deal_wq(0)]
+        x_q = []
         for a in range(PASSES):
-            wq_c.append(tile("wq_c%d" % a, [P, R], U32, offset=(0, 34 * KB)[a]))
-            deal(wq_c[a][:], wq_raw[a][:], 8)
-            woven = tile("x_woven0", [P, M, PACK], BF16, offset=4 * KB) if a == 0 else None
-            x_q.append(weave_and_quantise("x%d" % a, x_raw[a], woven))
+            x_woven = tile("x_woven%d" % a, [P, M, PACK], BF16, AT_X_WOVEN[a])
+            x_q.append(weave_and_quantise("x%d" % a, x_raw[a], x_woven))
+        wq_c.append(deal_wq(1))
         for b in range(PASSES):
-            kr_q[b, 1] = weave_and_quantise("kr%d1" % b, k_rows[b])
+            kr_woven = tile("k_woven%d1" % b, [P, BANK, PACK], BF16, AT_KR_WOVEN[b])
+            kr_q[b, 1] = weave_and_quantise("kr%d1" % b, k_rows[b], kr_woven)
 
         def query_passes(bank, a, b, blk):
-            cols = slice(blk * P, (blk + 1) * P)
+            m_cols = slice(blk * P, (blk + 1) * P)
             for t in range(PACK):
                 col = (b * PACK + t) * P
                 nc.tensor.matmul_mx(
-                    out=bank[:, t, :], lhsT=wq_c[a][:, col : col + P].bitcast(FP8X4),
+                    out=bank[:, t, :],
+                    lhsT=wq_c[b][:, a, t * P : (t + 1) * P].bitcast(FP8X4),
                     lhsT_scale=late_planes[:, a, col : col + P],
-                    rhs=x_q[a][0][:, cols].bitcast(FP8X4), rhs_scale=x_q[a][1][:, cols],
-                    start=(a == 0 and t == 0), stop=(a == PASSES - 1 and t == PACK - 1))
+                    rhs=x_q[a][0][:, m_cols].bitcast(FP8X4),
+                    rhs_scale=x_q[a][1][:, m_cols],
+                    start=(a == 0 and t == 0),
+                    stop=(a == PASSES - 1 and t == PACK - 1),
+                )
 
         qr_q = []
         for b in range(PASSES):
@@ -236,21 +295,26 @@ def tile_list_kvt_dl_scale_kernel(tc, tab_words, tab_scales, x, wq_words, wq_sca
                 query_passes(q_banks[blk], 0, b, blk)
             for blk in range(M // P):
                 query_passes(q_banks[blk], 1, b, blk)
-                nc.scalar.copy(q_woven[:, blk * P : (blk + 1) * P, :], q_banks[blk][:].rearrange("p t j -> p j t"))
+                weave_out_of_bank(q_woven, blk, q_banks[blk])
             qr_q.append(quantise("qr%d" % b, q_woven))
 
-        for nt in range(N // P):
-            values(nt, 1, True)
+        for nt, h in value_tiles[EARLY_VALUE_TILES:]:
+            values(nt, h, True)
 
         def scores(mt, h, c0, width, on_vector):
             bank = new_bank([P, width])
             m_cols = slice(mt * P, (mt + 1) * P)
-            cols = slice(c0, c0 + width)
+            j_cols = slice(c0, c0 + width)
             for b in range(PASSES):
                 nc.tensor.matmul_mx(
-                    out=bank[:], lhsT=qr_q[b][0][:, m_cols].bitcast(FP8X4), lhsT_scale=qr_q[b][1][:, m_cols],
-                    rhs=kr_q[b, h][0][:, cols].bitcast(FP8X4), rhs_scale=kr_q[b, h][1][:, cols],
-                    start=(b == 0), stop=(b == PASSES - 1))
+                    out=bank[:],
+                    lhsT=qr_q[b][0][:, m_cols].bitcast(FP8X4),
+                    lhsT_scale=qr_q[b][1][:, m_cols],
+                    rhs=kr_q[b, h][0][:, j_cols].bitcast(FP8X4),
+                    rhs_scale=kr_q[b, h][1][:, j_cols],
+                    start=(b == 0),
+                    stop=(b == PASSES - 1),
+                )
             res = outs.tile([P, width], F32, name="res")
             if on_vector:
                 nc.vector.tensor_scalar(res[:], bank[:], SCORE_SCALE, None, MULT)
@@ -261,5 +325,5 @@ def tile_list_kvt_dl_scale_kernel(tc, tab_words, tab_scales, x, wq_words, wq_sca
         score_tiles = [(mt, h) for mt in range(M // P) for h in range(HALVES)]
         for i, (mt, h) in enumerate(score_tiles[:-1]):
             scores(mt, h, 0, BANK, i % 2 == 1)
-        for half in range(2):
-            scores(*score_tiles[-1], half * BANK // 2, BANK // 2, half == 0)
+        for part in range(2):
+            scores(*score_tiles[-1], part * BANK // 2, BANK // 2, part == 0)

@@ -14,6 +14,7 @@ U8 = mybir.dt.uint8
 FP8X4 = mybir.dt.float8_e4m3fn_x4
 FP4X4 = mybir.dt.float4_e2m1fn_x4
 MULT = mybir.AluOpType.mult
+ADD = mybir.AluOpType.add
 COPY = mybir.ActivationFunctionType.Copy
 
 P = 128
@@ -31,25 +32,24 @@ SCORE_SCALE = 0.03125
 ALIGN = 64
 PSUM_BANKS = 8
 RESULT_TILES = 17
-EARLY_VALUE_TILES = 5
+PARTIAL_TILES = 4
 
 KB = 1024
 AT_TABLE = (32 * KB, 0)
-AT_PICKED_SCALES = 16 * KB - 512
-AT_LATE_ROWS = 16 * KB
-AT_LATE_RAW = 20 * KB
-AT_WK_CODES = 20 * KB
+AT_PICKED_SCALES = 0
+AT_WVD_RAW = (0, 8 * KB)
 AT_WK_RAW = 60 * KB
-AT_WV4_CODES = 60 * KB
-AT_WVD_RAW = (62 * KB, 26 * KB)
-AT_WQ_RAW = (34 * KB, 8 * KB)
-AT_X_RAW = (42 * KB, 12 * KB)
-AT_WVD_WOVEN = 0
-AT_KR_CODES = AT_WVD_RAW
-AT_X_WOVEN = (4 * KB, 38 * KB)
-AT_WQ_CODES = (0, 38 * KB)
-AT_KR_ROWS = (70 * KB, None)
-AT_KR_WOVEN = (8 * KB, 70 * KB)
+AT_WQ_RAW = (32 * KB, 62 * KB)
+AT_WQ_ROWS = 36 * KB
+AT_X_RAW = (40 * KB, 53 * KB)
+AT_WV4_CODES = (None, 61 * KB)
+AT_WVD_WOVEN = (None, 70 * KB)
+AT_X_WOVEN = (76 * KB, 80 * KB)
+AT_WQ_CODES = (None, 79 * KB)
+AT_KR_CODES = ((76 * KB, 83 * KB), (90 * KB, None))
+AT_Q_WOVEN = (86 * KB, 90 * KB)
+AT_QR_CODES = (70 * KB + 512, 72 * KB + 512)
+AT_KR_WOVEN = (66 * KB + 512, 86 * KB)
 
 
 def tile_list_kvt_dl_scale_kernel(
@@ -78,12 +78,12 @@ def tile_list_kvt_dl_scale_kernel(
             engine.memset(region.bitcast(I32), 0)
 
         def load_scale_rows(dst, src):
-            nc.sync.dma_start(dst.bitcast(I32), src.rearrange("a g w -> g a w").bitcast(I32))
+            nc.sync.dma_start(dst.bitcast(I32), src.rearrange("a g w -> (a g) w").bitcast(I32))
 
-        def spread_scale_rows(planes, staged):
-            for q in range(QUADS):
+        def spread_scale_rows(plane, staged, first):
+            for s in range(QUADS):
                 nc.sync.dma_start(
-                    planes[32 * q : 32 * q + 4].bitcast(I32), staged[8 * q : 8 * q + 8, :].bitcast(I32)
+                    plane[s:P:32, :].bitcast(I32), staged[first + s : first + BLOCKS : QUADS, :].bitcast(I32)
                 )
 
         def load_words(name, src, offset):
@@ -117,64 +117,95 @@ def tile_list_kvt_dl_scale_kernel(
             )
             return codes, scales
 
-        def weave_and_quantise(name, rows, woven):
+        def weave_and_quantise(name, rows, woven, offset=None):
             nc.vector.tensor_copy(
                 woven[:].rearrange("p (c i) t -> p c t i", i=LINE), rows[:].rearrange("p t (c i) -> p c t i", i=LINE)
             )
-            return quantise(name, woven)
+            return quantise(name, woven, offset)
 
         def weave_out_of_bank(woven, blk, bank):
             nc.scalar.copy(woven[:, blk * P : (blk + 1) * P, :], bank[:].rearrange("p t j -> p j t"))
+
+        def load_wv4(a):
+            codes = tile("wv4_c%d" % a, [P, 2 * N], U8, AT_WV4_CODES[a])
+            nc.sync.dma_start(codes[:].bitcast(I32), wv4_words[a].bitcast(I32))
+            return codes
 
         tab_s = tile("tab_s", [P, T], U8)
         load_scale_rows(tab_s[0:SCALE_ROWS, :], tab_scales)
         nc.sync.dma_start(offsets[:], offs)
         wk_s_raw = tile("wk_s_raw", [SCALE_ROWS, R], U8)
         load_scale_rows(wk_s_raw[:], wk_scales)
-        late_raw = tile("late_raw", [SCALE_ROWS, R + N], U8, AT_LATE_RAW)
-        load_scale_rows(late_raw[:, :R], wq_scales)
-        load_scale_rows(late_raw[:, R:], wv4_scales)
-        wk_raw = load_words("wk_raw", wk_words.rearrange("a p w -> p a w").bitcast(I32), AT_WK_RAW)
+        rows = tile("rows", [SCALE_ROWS, J + R + N], U8)
+        load_scale_rows(rows[:, J + R :], wv4_scales)
+        wq_s_raw = tile("wq_s_raw", [BLOCKS, PASSES, R], U8)
+        nc.sync.dma_start(wq_s_raw[:].bitcast(I32), wq_scales.rearrange("a g w -> g a w").bitcast(I32))
         tab_w = [load_table(0)]
+        wv4_c = [load_wv4(0)]
+        wk_raw = load_words("wk_raw", wk_words.rearrange("a p w -> p a w").bitcast(I32), AT_WK_RAW)
 
         zero(nc.vector, tab_s[32:64, :])
         zero(nc.gpsimd, tab_s[64:128, :])
-        planes = tile("planes", [P, PASSES, J + R], U8)
-        zero(nc.vector, planes[:].rearrange("p a w -> p (a w)"))
-        late_planes = tile("late_planes", [P, PASSES, R + N], U8)
-        zero(nc.gpsimd, late_planes[:].rearrange("p a w -> p (a w)"))
+        planes = [tile("planes%d" % a, [P, J + R + N], U8) for a in range(PASSES)]
+        zero(nc.vector, planes[0][:])
+        zero(nc.gpsimd, planes[1][:])
+        wq_plane = tile("wq_plane", [P, PASSES * R], U8)
+        zero(nc.gpsimd, wq_plane[:])
 
-        early_rows = tile("rows", [SCALE_ROWS, J + R], U8)
-        deal(early_rows[:, J:], wk_s_raw[:], 2)
+        deal(rows[:, J : J + R], wk_s_raw[:], 2)
         picked_scales = tile("picked_s", [P, J], U8, AT_PICKED_SCALES)
         nc.vector.tensor_copy(picked_scales[:], tab_s[:].indirect(offsets[:]))
-        nc.vector.tensor_copy(early_rows[:, :J].bitcast(I32), picked_scales[0:SCALE_ROWS, :].bitcast(I32))
-        spread_scale_rows(planes, early_rows)
+        nc.vector.tensor_copy(rows[:, :J].bitcast(I32), picked_scales[0:SCALE_ROWS, :].bitcast(I32))
+        spread_scale_rows(planes[0], rows, 0)
         tab_w.append(load_table(1))
-        late_rows = tile("late_rows", [SCALE_ROWS, R + N], U8, AT_LATE_ROWS)
-        deal(late_rows[:, :R], late_raw[:, :R], 2)
-        nc.vector.tensor_copy(late_rows[:, R:].bitcast(I32), late_raw[:, R:].bitcast(I32))
-        spread_scale_rows(late_planes, late_rows)
-        wk_c = tile("wk_c", [P, PASSES, 2 * R], U8, AT_WK_CODES)
-        deal(wk_c[:].rearrange("p a w -> p (a w)"), wk_raw[:].rearrange("p a w -> p (a w)"), 4)
-        wv4_c = tile("wv4_c", [P, PASSES, 2 * N], U8, AT_WV4_CODES)
-        nc.sync.dma_start(wv4_c[:].bitcast(I32), wv4_words.rearrange("a p w -> p a w").bitcast(I32))
-        wvd_raw = [load_f32("wvd", wvd, 0, AT_WVD_RAW[0])]
+        spread_scale_rows(planes[1], rows, BLOCKS)
 
         v_c, v_s = {}, {}
 
         def gather(a, h):
             entries = offsets[:, h * (BANK // LIST_ROWS) : (h + 1) * (BANK // LIST_ROWS)]
-            v_s[a, h] = planes[:, a, h * BANK : (h + 1) * BANK]
+            v_s[a, h] = planes[a][:, h * BANK : (h + 1) * BANK]
             v_c[a, h] = tile("v_c%d%d" % (a, h), [P, BANK], U32)
             nc.vector.tensor_copy(v_c[a, h][:], tab_w[a][:].bitcast(U32).indirect(entries))
+
+        gather(0, 0)
+        gather(0, 1)
+        wq_raw = [load_wq(0)]
+        x_raw = [load_f32("x", x, 0, AT_X_RAW[0])]
+        wq_rows = tile("wq_rows", [BLOCKS, PASSES * R], U8, AT_WQ_ROWS)
+        deal(wq_rows[:], wq_s_raw[:].rearrange("p a w -> p (a w)"), 2)
+        spread_scale_rows(wq_plane, wq_rows, 0)
+        wk_c = tile("wk_c", [P, PASSES, 2 * R], U8)
+        deal(wk_c[:].rearrange("p a w -> p (a w)"), wk_raw[:].rearrange("p a w -> p (a w)"), 4)
+        x_raw.append(load_f32("x", x, 1, AT_X_RAW[1]))
+        wq_raw.append(load_wq(1))
+        wv4_c.append(load_wv4(1))
+
+        def base_pass(bank, a, nt, h, start, stop):
+            nc.tensor.matmul_mx(
+                out=bank[:],
+                lhsT=wv4_c[a][:, 2 * nt * P : 2 * (nt + 1) * P].bitcast(FP4X4),
+                lhsT_scale=planes[a][:, J + R + nt * P : J + R + (nt + 1) * P],
+                rhs=v_c[a, h][:].bitcast(FP8X4),
+                rhs_scale=v_s[a, h],
+                start=start,
+                stop=stop,
+            )
+
+        value_tiles = [(nt, h) for h in range(HALVES) for nt in range(N // P)]
+        partial = {}
+        for nt, h in value_tiles[:PARTIAL_TILES]:
+            bank = new_bank([P, BANK])
+            base_pass(bank, 0, nt, h, True, True)
+            partial[nt, h] = tile("partial%d%d" % (nt, h), [P, BANK], F32)
+            nc.scalar.copy(partial[nt, h][:], bank[:])
 
         def key_pass(out, a, b, t, h, cols, start, stop):
             col = (b * PACK + t) * P
             nc.tensor.matmul_mx(
                 out=out,
                 lhsT=wk_c[:, a, 2 * col : 2 * (col + P)].bitcast(FP4X4),
-                lhsT_scale=planes[:, a, J + col : J + col + P],
+                lhsT_scale=planes[a][:, J + col : J + col + P],
                 rhs=v_c[a, h][:, cols].bitcast(FP8X4),
                 rhs_scale=v_s[a, h][:, cols],
                 start=start,
@@ -188,19 +219,13 @@ def tile_list_kvt_dl_scale_kernel(
                 first, last = a == 0 and t == 0, a == PASSES - 1 and t == PACK - 1
                 key_pass(k_banks[b, blk][:, t, :], a, b, t, 0, slice(blk * P, (blk + 1) * P), first, last)
 
-        gather(0, 0)
-        gather(0, 1)
-        wvd_raw.append(load_f32("wvd", wvd, 1, AT_WVD_RAW[1]))
-        wq_raw = [load_wq(0)]
-        x_raw = [load_f32("x", x, 0, AT_X_RAW[0])]
         for b in range(PASSES):
             for blk in range(BANK // P):
                 k_banks[b, blk] = new_bank([P, PACK, P])
                 narrow_key_passes(0, b, blk)
         gather(1, 0)
         gather(1, 1)
-        x_raw.append(load_f32("x", x, 1, AT_X_RAW[1]))
-        wq_raw.append(load_wq(1))
+        wvd_raw = [load_f32("wvd", wvd, a, AT_WVD_RAW[a]) for a in range(PASSES)]
         k_woven = []
         for b in range(PASSES):
             k_woven.append(tile("k_woven%d" % b, [P, BANK, PACK], BF16))
@@ -210,53 +235,12 @@ def tile_list_kvt_dl_scale_kernel(
 
         k_rows = []
         for b in range(PASSES):
-            k_rows.append(tile("k_rows%d" % b, [P, PACK, BANK], BF16, AT_KR_ROWS[b]))
+            k_rows.append(tile("k_rows%d" % b, [P, PACK, BANK], BF16))
             for t in range(PACK):
                 bank = new_bank([P, BANK])
                 for a in range(PASSES):
                     key_pass(bank[:], a, b, t, 1, slice(0, BANK), a == 0, a == PASSES - 1)
                 nc.scalar.copy(k_rows[b][:, t, :], bank[:])
-
-        wvd_q, kr_q = {}, {}
-        wvd_woven = tile("wvd_woven", [P, PASSES, N, PACK], BF16, AT_WVD_WOVEN)
-        for a in range(PASSES):
-            wvd_q[a] = weave_and_quantise("wvd%d" % a, wvd_raw[a], wvd_woven[:, a])
-        for b in range(PASSES):
-            kr_q[b, 0] = quantise("kr%d0" % b, k_woven[b], AT_KR_CODES[b])
-
-        def values(nt, h, on_vector):
-            bank = new_bank([P, BANK])
-            n_cols = slice(nt * P, (nt + 1) * P)
-            for a in range(PASSES):
-                nc.tensor.matmul_mx(
-                    out=bank[:],
-                    lhsT=wv4_c[:, a, 2 * nt * P : 2 * (nt + 1) * P].bitcast(FP4X4),
-                    lhsT_scale=late_planes[:, a, R + nt * P : R + (nt + 1) * P],
-                    rhs=v_c[a, h][:].bitcast(FP8X4),
-                    rhs_scale=v_s[a, h],
-                    start=(a == 0),
-                    stop=False,
-                )
-            for a in range(PASSES):
-                nc.tensor.matmul_mx(
-                    out=bank[:],
-                    lhsT=wvd_q[a][0][:, n_cols].bitcast(FP8X4),
-                    lhsT_scale=wvd_q[a][1][:, n_cols],
-                    rhs=v_c[a, h][:].bitcast(FP8X4),
-                    rhs_scale=v_s[a, h],
-                    start=False,
-                    stop=(a == PASSES - 1),
-                )
-            res = outs.tile([P, BANK], F32, name="res")
-            if on_vector:
-                nc.vector.tensor_copy(res[:], bank[:])
-            else:
-                nc.scalar.copy(res[:], bank[:])
-            nc.sync.dma_start(out_1[n_cols, h * BANK : (h + 1) * BANK], res[:])
-
-        value_tiles = [(nt, h) for h in range(HALVES) for nt in range(N // P)]
-        for nt, h in value_tiles[:EARLY_VALUE_TILES]:
-            values(nt, h, False)
 
         def deal_wq(b):
             codes = tile("wq_c%d" % b, [P, PASSES, K_PASS], U32, AT_WQ_CODES[b])
@@ -269,37 +253,69 @@ def tile_list_kvt_dl_scale_kernel(
             x_woven = tile("x_woven%d" % a, [P, M, PACK], BF16, AT_X_WOVEN[a])
             x_q.append(weave_and_quantise("x%d" % a, x_raw[a], x_woven))
         wq_c.append(deal_wq(1))
-        for b in range(PASSES):
-            kr_woven = tile("k_woven%d1" % b, [P, BANK, PACK], BF16, AT_KR_WOVEN[b])
-            kr_q[b, 1] = weave_and_quantise("kr%d1" % b, k_rows[b], kr_woven)
 
         def query_passes(bank, a, b, blk):
             m_cols = slice(blk * P, (blk + 1) * P)
             for t in range(PACK):
-                col = (b * PACK + t) * P
+                col = a * R + (b * PACK + t) * P
                 nc.tensor.matmul_mx(
                     out=bank[:, t, :],
                     lhsT=wq_c[b][:, a, t * P : (t + 1) * P].bitcast(FP8X4),
-                    lhsT_scale=late_planes[:, a, col : col + P],
+                    lhsT_scale=wq_plane[:, col : col + P],
                     rhs=x_q[a][0][:, m_cols].bitcast(FP8X4),
                     rhs_scale=x_q[a][1][:, m_cols],
                     start=(a == 0 and t == 0),
                     stop=(a == PASSES - 1 and t == PACK - 1),
                 )
 
-        qr_q = []
+        q_woven = []
         for b in range(PASSES):
-            q_woven = tile("q_woven%d" % b, [P, M, PACK], BF16)
+            q_woven.append(tile("q_woven%d" % b, [P, M, PACK], BF16, AT_Q_WOVEN[b]))
             q_banks = [new_bank([P, PACK, P]) for blk in range(M // P)]
             for blk in range(M // P):
                 query_passes(q_banks[blk], 0, b, blk)
             for blk in range(M // P):
                 query_passes(q_banks[blk], 1, b, blk)
-                weave_out_of_bank(q_woven, blk, q_banks[blk])
-            qr_q.append(quantise("qr%d" % b, q_woven))
+                weave_out_of_bank(q_woven[b], blk, q_banks[blk])
 
-        for nt, h in value_tiles[EARLY_VALUE_TILES:]:
-            values(nt, h, True)
+        wvd_q, kr_q = {}, {}
+        for a in range(PASSES):
+            wvd_woven = tile("wvd_woven%d" % a, [P, N, PACK], BF16, AT_WVD_WOVEN[a])
+            wvd_q[a] = weave_and_quantise("wvd%d" % a, wvd_raw[a], wvd_woven)
+        qr_q = [quantise("qr%d" % b, q_woven[b], AT_QR_CODES[b]) for b in range(PASSES)]
+        for b in range(PASSES):
+            kr_q[b, 0] = quantise("kr%d0" % b, k_woven[b], AT_KR_CODES[0][b])
+        for b in range(PASSES):
+            kr_woven = tile("k_woven%d1" % b, [P, BANK, PACK], BF16, AT_KR_WOVEN[b])
+            kr_q[b, 1] = weave_and_quantise("kr%d1" % b, k_rows[b], kr_woven, AT_KR_CODES[1][b])
+
+        def change_pass(bank, a, nt, h):
+            n_cols = slice(nt * P, (nt + 1) * P)
+            nc.tensor.matmul_mx(
+                out=bank[:],
+                lhsT=wvd_q[a][0][:, n_cols].bitcast(FP8X4),
+                lhsT_scale=wvd_q[a][1][:, n_cols],
+                rhs=v_c[a, h][:].bitcast(FP8X4),
+                rhs_scale=v_s[a, h],
+                start=False,
+                stop=(a == PASSES - 1),
+            )
+
+        def values(group):
+            banks = [new_bank([P, BANK]) for nt_h in group]
+            for bank, (nt, h) in zip(banks, group):
+                first = 1 if (nt, h) in partial else 0
+                for a in range(first, PASSES):
+                    base_pass(bank, a, nt, h, a == first, False)
+                change_pass(bank, 0, nt, h)
+            for bank, (nt, h) in zip(banks, group):
+                change_pass(bank, 1, nt, h)
+                res = outs.tile([P, BANK], F32, name="res")
+                if (nt, h) in partial:
+                    nc.vector.tensor_tensor(res[:], bank[:], partial[nt, h][:], ADD)
+                else:
+                    nc.scalar.copy(res[:], bank[:])
+                nc.sync.dma_start(out_1[nt * P : (nt + 1) * P, h * BANK : (h + 1) * BANK], res[:])
 
         def scores(mt, h, c0, width, on_vector):
             bank = new_bank([P, width])
@@ -322,8 +338,16 @@ def tile_list_kvt_dl_scale_kernel(
                 nc.scalar.activation(res[:], bank[:], COPY, scale=SCORE_SCALE)
             nc.sync.dma_start(out_0[m_cols, h * BANK + c0 : h * BANK + c0 + width], res[:])
 
-        score_tiles = [(mt, h) for mt in range(M // P) for h in range(HALVES)]
-        for i, (mt, h) in enumerate(score_tiles[:-1]):
-            scores(mt, h, 0, BANK, i % 2 == 1)
+        values([(0, 1), (1, 1)])
+        values([(2, 1)])
+        scores(0, 0, 0, BANK, False)
+        scores(1, 0, 0, BANK, False)
+        values([(3, 1)])
+        scores(2, 0, 0, BANK, False)
+        scores(3, 0, 0, BANK, False)
+        for i in range(M // P):
+            values([(i, 0)])
+            if i < M // P - 1:
+                scores(i, 1, 0, BANK, False)
         for part in range(2):
-            scores(*score_tiles[-1], part * BANK // 2, BANK // 2, part == 0)
+            scores(M // P - 1, 1, part * BANK // 2, BANK // 2, part == 1)

@@ -32,24 +32,27 @@ SCORE_SCALE = 0.03125
 ALIGN = 64
 PSUM_BANKS = 8
 RESULT_TILES = 17
-PARTIAL_TILES = 4
+PARTIAL_TILES = 6
 
 KB = 1024
 AT_TABLE = (32 * KB, 0)
-AT_PICKED_SCALES = 0
-AT_WVD_RAW = (0, 8 * KB)
-AT_WK_RAW = 60 * KB
-AT_WQ_RAW = (32 * KB, 62 * KB)
-AT_WQ_ROWS = 36 * KB
-AT_X_RAW = (40 * KB, 53 * KB)
-AT_WV4_CODES = (None, 61 * KB)
-AT_WVD_WOVEN = (None, 70 * KB)
-AT_X_WOVEN = (76 * KB, 80 * KB)
+AT_PICKED_SCALES = 16 * KB - 512
+AT_WVD_RAW = (0, 9 * KB)
+AT_WK_RAW = (None, 16 * KB)
+AT_WQ_S_RAW = 62 * KB
+AT_WQ_RAW = (33 * KB, 62 * KB)
+AT_WQ_ROWS = 58 * KB
+AT_WK0 = 58 * KB
+AT_LAST_WORDS = 17 * KB
+AT_X_RAW = (40 * KB, 25 * KB)
+AT_WV4_CODES = (None, 8 * KB)
+AT_WVD_WOVEN = ((None, None), (70 * KB, None))
+AT_X_WOVEN = ((None, None), (80 * KB, 82 * KB))
 AT_WQ_CODES = (None, 79 * KB)
-AT_KR_CODES = ((76 * KB, 83 * KB), (90 * KB, None))
+AT_KR_CODES = ((None, 83 * KB), (90 * KB, None))
 AT_Q_WOVEN = (86 * KB, 90 * KB)
-AT_QR_CODES = (70 * KB + 512, 72 * KB + 512)
-AT_KR_WOVEN = (66 * KB + 512, 86 * KB)
+AT_QR_CODES = (69 * KB, 71 * KB)
+AT_KR_WOVEN = (64 * KB, 86 * KB)
 
 
 def tile_list_kvt_dl_scale_kernel(
@@ -110,8 +113,8 @@ def tile_list_kvt_dl_scale_kernel(
             )
 
         def quantise(name, woven, offset=None):
-            codes = tile(name + "_c", [P, BANK], U32, offset)
-            scales = tile(name + "_s", [P, BANK], U8)
+            codes = tile(name + "_c", [P, woven.shape[1]], U32, offset)
+            scales = tile(name + "_s", [P, woven.shape[1]], U8)
             nc.vector.quantize_mx(
                 out=codes[:].bitcast(FP8X4), scales=scales[:], in_=woven[:].rearrange("p j t -> p (j t)")
             )
@@ -119,12 +122,21 @@ def tile_list_kvt_dl_scale_kernel(
 
         def weave_and_quantise(name, rows, woven, offset=None):
             nc.vector.tensor_copy(
-                woven[:].rearrange("p (c i) t -> p c t i", i=LINE), rows[:].rearrange("p t (c i) -> p c t i", i=LINE)
+                woven[:].rearrange("p (c i) t -> p c t i", i=LINE), rows.rearrange("p t (c i) -> p c t i", i=LINE)
             )
             return quantise(name, woven, offset)
 
-        def weave_out_of_bank(woven, blk, bank):
-            nc.scalar.copy(woven[:, blk * P : (blk + 1) * P, :], bank[:].rearrange("p t j -> p j t"))
+        def quantise_by_halves(name, raw, offsets_woven):
+            halves = []
+            for part in range(2):
+                woven = tile("%s_woven%d" % (name, part), [P, BANK // 2, PACK], BF16, offsets_woven[part])
+                cols = slice(part * BANK // 2, (part + 1) * BANK // 2)
+                halves.append(weave_and_quantise("%s_%d" % (name, part), raw[:, :, cols], woven))
+            return halves
+
+        def weave_out_of_bank(woven, blk, bank, on_vector=False):
+            copy = nc.vector.tensor_copy if on_vector else nc.scalar.copy
+            copy(woven[:, blk * P : (blk + 1) * P, :], bank[:].rearrange("p t j -> p j t"))
 
         def load_wv4(a):
             codes = tile("wv4_c%d" % a, [P, 2 * N], U8, AT_WV4_CODES[a])
@@ -138,11 +150,11 @@ def tile_list_kvt_dl_scale_kernel(
         load_scale_rows(wk_s_raw[:], wk_scales)
         rows = tile("rows", [SCALE_ROWS, J + R + N], U8)
         load_scale_rows(rows[:, J + R :], wv4_scales)
-        wq_s_raw = tile("wq_s_raw", [BLOCKS, PASSES, R], U8)
+        wq_s_raw = tile("wq_s_raw", [BLOCKS, PASSES, R], U8, AT_WQ_S_RAW)
         nc.sync.dma_start(wq_s_raw[:].bitcast(I32), wq_scales.rearrange("a g w -> g a w").bitcast(I32))
         tab_w = [load_table(0)]
         wv4_c = [load_wv4(0)]
-        wk_raw = load_words("wk_raw", wk_words.rearrange("a p w -> p a w").bitcast(I32), AT_WK_RAW)
+        wk_raw = [load_words("wk_raw0", wk_words[0].bitcast(I32), AT_WK0)]
 
         zero(nc.vector, tab_s[32:64, :])
         zero(nc.gpsimd, tab_s[64:128, :])
@@ -158,28 +170,27 @@ def tile_list_kvt_dl_scale_kernel(
         nc.vector.tensor_copy(rows[:, :J].bitcast(I32), picked_scales[0:SCALE_ROWS, :].bitcast(I32))
         spread_scale_rows(planes[0], rows, 0)
         tab_w.append(load_table(1))
+        wk_raw.append(load_words("wk_raw1", wk_words[1].bitcast(I32), AT_WK_RAW[1]))
         spread_scale_rows(planes[1], rows, BLOCKS)
 
         v_c, v_s = {}, {}
 
-        def gather(a, h):
+        def gather(a, h, offset=None):
             entries = offsets[:, h * (BANK // LIST_ROWS) : (h + 1) * (BANK // LIST_ROWS)]
             v_s[a, h] = planes[a][:, h * BANK : (h + 1) * BANK]
-            v_c[a, h] = tile("v_c%d%d" % (a, h), [P, BANK], U32)
+            v_c[a, h] = tile("v_c%d%d" % (a, h), [P, BANK], U32, offset)
             nc.vector.tensor_copy(v_c[a, h][:], tab_w[a][:].bitcast(U32).indirect(entries))
 
         gather(0, 0)
         gather(0, 1)
         wq_raw = [load_wq(0)]
-        x_raw = [load_f32("x", x, 0, AT_X_RAW[0])]
+        x_raw = [load_f32("x", x, a, AT_X_RAW[a]) for a in range(PASSES)]
+        wk_c = [tile("wk_c%d" % a, [P, 2 * R], U8) for a in range(PASSES)]
+        deal(wk_c[0][:], wk_raw[0][:], 4)
         wq_rows = tile("wq_rows", [BLOCKS, PASSES * R], U8, AT_WQ_ROWS)
         deal(wq_rows[:], wq_s_raw[:].rearrange("p a w -> p (a w)"), 2)
         spread_scale_rows(wq_plane, wq_rows, 0)
-        wk_c = tile("wk_c", [P, PASSES, 2 * R], U8)
-        deal(wk_c[:].rearrange("p a w -> p (a w)"), wk_raw[:].rearrange("p a w -> p (a w)"), 4)
-        x_raw.append(load_f32("x", x, 1, AT_X_RAW[1]))
         wq_raw.append(load_wq(1))
-        wv4_c.append(load_wv4(1))
 
         def base_pass(bank, a, nt, h, start, stop):
             nc.tensor.matmul_mx(
@@ -192,7 +203,7 @@ def tile_list_kvt_dl_scale_kernel(
                 stop=stop,
             )
 
-        value_tiles = [(nt, h) for h in range(HALVES) for nt in range(N // P)]
+        value_tiles = [(nt, 0) for nt in range(N // P)] + [(nt, 1) for nt in reversed(range(N // P))]
         partial = {}
         for nt, h in value_tiles[:PARTIAL_TILES]:
             bank = new_bank([P, BANK])
@@ -204,7 +215,7 @@ def tile_list_kvt_dl_scale_kernel(
             col = (b * PACK + t) * P
             nc.tensor.matmul_mx(
                 out=out,
-                lhsT=wk_c[:, a, 2 * col : 2 * (col + P)].bitcast(FP4X4),
+                lhsT=wk_c[a][:, 2 * col : 2 * (col + P)].bitcast(FP4X4),
                 lhsT_scale=planes[a][:, J + col : J + col + P],
                 rhs=v_c[a, h][:, cols].bitcast(FP8X4),
                 rhs_scale=v_s[a, h][:, cols],
@@ -224,14 +235,16 @@ def tile_list_kvt_dl_scale_kernel(
                 k_banks[b, blk] = new_bank([P, PACK, P])
                 narrow_key_passes(0, b, blk)
         gather(1, 0)
-        gather(1, 1)
+        deal(wk_c[1][:], wk_raw[1][:], 4)
+        gather(1, 1, AT_LAST_WORDS)
         wvd_raw = [load_f32("wvd", wvd, a, AT_WVD_RAW[a]) for a in range(PASSES)]
+        wv4_c.append(load_wv4(1))
         k_woven = []
         for b in range(PASSES):
             k_woven.append(tile("k_woven%d" % b, [P, BANK, PACK], BF16))
             for blk in range(BANK // P):
                 narrow_key_passes(1, b, blk)
-                weave_out_of_bank(k_woven[b], blk, k_banks[b, blk])
+                weave_out_of_bank(k_woven[b], blk, k_banks[b, blk], (b, blk) in ((0, 3), (1, 1)))
 
         k_rows = []
         for b in range(PASSES):
@@ -250,20 +263,20 @@ def tile_list_kvt_dl_scale_kernel(
         wq_c = [deal_wq(0)]
         x_q = []
         for a in range(PASSES):
-            x_woven = tile("x_woven%d" % a, [P, M, PACK], BF16, AT_X_WOVEN[a])
-            x_q.append(weave_and_quantise("x%d" % a, x_raw[a], x_woven))
+            x_q.append(quantise_by_halves("x%d" % a, x_raw[a], AT_X_WOVEN[a]))
         wq_c.append(deal_wq(1))
 
         def query_passes(bank, a, b, blk):
-            m_cols = slice(blk * P, (blk + 1) * P)
+            x_codes, x_plane = x_q[a][blk // 2]
+            m_cols = slice(blk % 2 * P, (blk % 2 + 1) * P)
             for t in range(PACK):
                 col = a * R + (b * PACK + t) * P
                 nc.tensor.matmul_mx(
                     out=bank[:, t, :],
                     lhsT=wq_c[b][:, a, t * P : (t + 1) * P].bitcast(FP8X4),
                     lhsT_scale=wq_plane[:, col : col + P],
-                    rhs=x_q[a][0][:, m_cols].bitcast(FP8X4),
-                    rhs_scale=x_q[a][1][:, m_cols],
+                    rhs=x_codes[:, m_cols].bitcast(FP8X4),
+                    rhs_scale=x_plane[:, m_cols],
                     start=(a == 0 and t == 0),
                     stop=(a == PASSES - 1 and t == PACK - 1),
                 )
@@ -280,42 +293,45 @@ def tile_list_kvt_dl_scale_kernel(
 
         wvd_q, kr_q = {}, {}
         for a in range(PASSES):
-            wvd_woven = tile("wvd_woven%d" % a, [P, N, PACK], BF16, AT_WVD_WOVEN[a])
-            wvd_q[a] = weave_and_quantise("wvd%d" % a, wvd_raw[a], wvd_woven)
+            wvd_q[a] = quantise_by_halves("wvd%d" % a, wvd_raw[a], AT_WVD_WOVEN[a])
         qr_q = [quantise("qr%d" % b, q_woven[b], AT_QR_CODES[b]) for b in range(PASSES)]
         for b in range(PASSES):
             kr_q[b, 0] = quantise("kr%d0" % b, k_woven[b], AT_KR_CODES[0][b])
         for b in range(PASSES):
             kr_woven = tile("k_woven%d1" % b, [P, BANK, PACK], BF16, AT_KR_WOVEN[b])
-            kr_q[b, 1] = weave_and_quantise("kr%d1" % b, k_rows[b], kr_woven, AT_KR_CODES[1][b])
+            kr_q[b, 1] = weave_and_quantise("kr%d1" % b, k_rows[b][:], kr_woven, AT_KR_CODES[1][b])
 
-        def change_pass(bank, a, nt, h):
-            n_cols = slice(nt * P, (nt + 1) * P)
+        def change_pass(bank, a, nt, h, start):
+            codes, plane = wvd_q[a][nt // 2]
+            n_cols = slice(nt % 2 * P, (nt % 2 + 1) * P)
             nc.tensor.matmul_mx(
                 out=bank[:],
-                lhsT=wvd_q[a][0][:, n_cols].bitcast(FP8X4),
-                lhsT_scale=wvd_q[a][1][:, n_cols],
+                lhsT=codes[:, n_cols].bitcast(FP8X4),
+                lhsT_scale=plane[:, n_cols],
                 rhs=v_c[a, h][:].bitcast(FP8X4),
                 rhs_scale=v_s[a, h],
-                start=False,
+                start=start,
                 stop=(a == PASSES - 1),
             )
 
-        def values(group):
-            banks = [new_bank([P, BANK]) for nt_h in group]
-            for bank, (nt, h) in zip(banks, group):
-                first = 1 if (nt, h) in partial else 0
-                for a in range(first, PASSES):
-                    base_pass(bank, a, nt, h, a == first, False)
-                change_pass(bank, 0, nt, h)
-            for bank, (nt, h) in zip(banks, group):
-                change_pass(bank, 1, nt, h)
-                res = outs.tile([P, BANK], F32, name="res")
-                if (nt, h) in partial:
-                    nc.vector.tensor_tensor(res[:], bank[:], partial[nt, h][:], ADD)
+        def values(nt, h, pieces=1):
+            bank = new_bank([P, BANK])
+            begun = (nt, h) in partial
+            if not begun:
+                base_pass(bank, 0, nt, h, True, False)
+            change_pass(bank, 0, nt, h, begun)
+            base_pass(bank, 1, nt, h, False, False)
+            change_pass(bank, 1, nt, h, False)
+            width = BANK // pieces
+            for piece in range(pieces):
+                cols = slice(piece * width, (piece + 1) * width)
+                res = outs.tile([P, width], F32, name="res")
+                if begun:
+                    nc.vector.tensor_tensor(res[:], bank[:, cols], partial[nt, h][:, cols], ADD)
                 else:
-                    nc.scalar.copy(res[:], bank[:])
-                nc.sync.dma_start(out_1[nt * P : (nt + 1) * P, h * BANK : (h + 1) * BANK], res[:])
+                    nc.scalar.copy(res[:], bank[:, cols])
+                c0 = h * BANK + piece * width
+                nc.sync.dma_start(out_1[nt * P : (nt + 1) * P, c0 : c0 + width], res[:])
 
         def scores(mt, h, c0, width, on_vector):
             bank = new_bank([P, width])
@@ -338,16 +354,12 @@ def tile_list_kvt_dl_scale_kernel(
                 nc.scalar.activation(res[:], bank[:], COPY, scale=SCORE_SCALE)
             nc.sync.dma_start(out_0[m_cols, h * BANK + c0 : h * BANK + c0 + width], res[:])
 
-        values([(0, 1), (1, 1)])
-        values([(2, 1)])
-        scores(0, 0, 0, BANK, False)
-        scores(1, 0, 0, BANK, False)
-        values([(3, 1)])
-        scores(2, 0, 0, BANK, False)
-        scores(3, 0, 0, BANK, False)
+        values(0, 1)
+        values(1, 1)
+        for mt in range(M // P):
+            scores(mt, 0, 0, BANK, False)
+        values(2, 1)
         for i in range(M // P):
-            values([(i, 0)])
-            if i < M // P - 1:
-                scores(i, 1, 0, BANK, False)
-        for part in range(2):
-            scores(M // P - 1, 1, part * BANK // 2, BANK // 2, part == 1)
+            values(i, 0)
+            scores(i, 1, 0, BANK, False)
+        values(3, 1, 2)

@@ -49,10 +49,10 @@ AT_WV4_CODES = (None, 8 * KB)
 AT_WVD_WOVEN = ((None, None), (70 * KB, None))
 AT_X_WOVEN = ((None, None), (80 * KB, 82 * KB))
 AT_WQ_CODES = (None, 79 * KB)
-AT_KR_CODES = ((None, 83 * KB), (90 * KB, None))
+AT_KR_CODES = ((None, 83 * KB), (90 * KB, 92 * KB))
 AT_Q_WOVEN = (86 * KB, 90 * KB)
 AT_QR_CODES = (69 * KB, 71 * KB)
-AT_KR_WOVEN = (64 * KB, 86 * KB)
+AT_KR_WOVEN = (64 * KB, 92 * KB)
 
 
 def tile_list_kvt_dl_scale_kernel(
@@ -225,10 +225,10 @@ def tile_list_kvt_dl_scale_kernel(
 
         k_banks = {}
 
-        def narrow_key_passes(a, b, blk):
+        def narrow_key_passes(a, b, blk, h=0):
             for t in range(PACK):
                 first, last = a == 0 and t == 0, a == PASSES - 1 and t == PACK - 1
-                key_pass(k_banks[b, blk][:, t, :], a, b, t, 0, slice(blk * P, (blk + 1) * P), first, last)
+                key_pass(k_banks[b, blk][:, t, :], a, b, t, h, slice(blk * P, (blk + 1) * P), first, last)
 
         for b in range(PASSES):
             for blk in range(BANK // P):
@@ -246,14 +246,14 @@ def tile_list_kvt_dl_scale_kernel(
                 narrow_key_passes(1, b, blk)
                 weave_out_of_bank(k_woven[b], blk, k_banks[b, blk], (b, blk) in ((0, 3), (1, 1)))
 
-        k_rows = []
+        k_late = []
         for b in range(PASSES):
-            k_rows.append(tile("k_rows%d" % b, [P, PACK, BANK], BF16))
-            for t in range(PACK):
-                bank = new_bank([P, BANK])
+            k_late.append(tile("k_late%d" % b, [P, BANK, PACK], BF16))
+            for blk in range(BANK // P):
+                k_banks[b, blk] = new_bank([P, PACK, P])
                 for a in range(PASSES):
-                    key_pass(bank[:], a, b, t, 1, slice(0, BANK), a == 0, a == PASSES - 1)
-                nc.scalar.copy(k_rows[b][:, t, :], bank[:])
+                    narrow_key_passes(a, b, blk, 1)
+                weave_out_of_bank(k_late[b], blk, k_banks[b, blk])
 
         def deal_wq(b):
             codes = tile("wq_c%d" % b, [P, PASSES, K_PASS], U32, AT_WQ_CODES[b])
@@ -298,8 +298,7 @@ def tile_list_kvt_dl_scale_kernel(
         for b in range(PASSES):
             kr_q[b, 0] = quantise("kr%d0" % b, k_woven[b], AT_KR_CODES[0][b])
         for b in range(PASSES):
-            kr_woven = tile("k_woven%d1" % b, [P, BANK, PACK], BF16, AT_KR_WOVEN[b])
-            kr_q[b, 1] = weave_and_quantise("kr%d1" % b, k_rows[b][:], kr_woven, AT_KR_CODES[1][b])
+            kr_q[b, 1] = quantise("kr%d1" % b, k_late[b], AT_KR_CODES[1][b])
 
         def change_pass(bank, a, nt, h, start):
             codes, plane = wvd_q[a][nt // 2]

@@ -32,7 +32,7 @@ SCORE_SCALE = 0.03125
 ALIGN = 64
 PSUM_BANKS = 8
 RESULT_TILES = 17
-PARTIAL_TILES = 6
+PARTIAL_TILES = 7
 
 KB = 1024
 AT_TABLE = (32 * KB, 0)
@@ -46,10 +46,10 @@ AT_WK0 = 58 * KB
 AT_LAST_WORDS = 17 * KB
 AT_X_RAW = (40 * KB, 25 * KB)
 AT_WV4_CODES = (None, 8 * KB)
-AT_WVD_WOVEN = ((None, None), (70 * KB, None))
+AT_WVD_WOVEN = ((None, None), (70 * KB, 92 * KB))
 AT_X_WOVEN = ((None, None), (80 * KB, 82 * KB))
 AT_WQ_CODES = (None, 79 * KB)
-AT_KR_CODES = ((None, 83 * KB), (90 * KB, 92 * KB))
+AT_KR_CODES = ((None, 83 * KB), (88 * KB, 90 * KB))
 AT_Q_WOVEN = (86 * KB, 90 * KB)
 AT_QR_CODES = (69 * KB, 71 * KB)
 AT_KR_WOVEN = (64 * KB, 92 * KB)
@@ -126,13 +126,10 @@ def tile_list_kvt_dl_scale_kernel(
             )
             return quantise(name, woven, offset)
 
-        def quantise_by_halves(name, raw, offsets_woven):
-            halves = []
-            for part in range(2):
-                woven = tile("%s_woven%d" % (name, part), [P, BANK // 2, PACK], BF16, offsets_woven[part])
-                cols = slice(part * BANK // 2, (part + 1) * BANK // 2)
-                halves.append(weave_and_quantise("%s_%d" % (name, part), raw[:, :, cols], woven))
-            return halves
+        def quantise_half(name, raw, part, offset_woven):
+            woven = tile("%s_woven%d" % (name, part), [P, BANK // 2, PACK], BF16, offset_woven)
+            cols = slice(part * BANK // 2, (part + 1) * BANK // 2)
+            return weave_and_quantise("%s_%d" % (name, part), raw[:, :, cols], woven)
 
         def weave_out_of_bank(woven, blk, bank, on_vector=False):
             copy = nc.vector.tensor_copy if on_vector else nc.scalar.copy
@@ -192,13 +189,13 @@ def tile_list_kvt_dl_scale_kernel(
         spread_scale_rows(wq_plane, wq_rows, 0)
         wq_raw.append(load_wq(1))
 
-        def base_pass(bank, a, nt, h, start, stop):
+        def base_pass(out, a, nt, h, start, stop, cols=slice(0, BANK)):
             nc.tensor.matmul_mx(
-                out=bank[:],
+                out=out,
                 lhsT=wv4_c[a][:, 2 * nt * P : 2 * (nt + 1) * P].bitcast(FP4X4),
                 lhsT_scale=planes[a][:, J + R + nt * P : J + R + (nt + 1) * P],
-                rhs=v_c[a, h][:].bitcast(FP8X4),
-                rhs_scale=v_s[a, h],
+                rhs=v_c[a, h][:, cols].bitcast(FP8X4),
+                rhs_scale=v_s[a, h][:, cols],
                 start=start,
                 stop=stop,
             )
@@ -207,7 +204,7 @@ def tile_list_kvt_dl_scale_kernel(
         partial = {}
         for nt, h in value_tiles[:PARTIAL_TILES]:
             bank = new_bank([P, BANK])
-            base_pass(bank, 0, nt, h, True, True)
+            base_pass(bank[:], 0, nt, h, True, True)
             partial[nt, h] = tile("partial%d%d" % (nt, h), [P, BANK], F32)
             nc.scalar.copy(partial[nt, h][:], bank[:])
 
@@ -263,7 +260,7 @@ def tile_list_kvt_dl_scale_kernel(
         wq_c = [deal_wq(0)]
         x_q = []
         for a in range(PASSES):
-            x_q.append(quantise_by_halves("x%d" % a, x_raw[a], AT_X_WOVEN[a]))
+            x_q.append([quantise_half("x%d" % a, x_raw[a], part, AT_X_WOVEN[a][part]) for part in range(2)])
         wq_c.append(deal_wq(1))
 
         def query_passes(bank, a, b, blk):
@@ -292,45 +289,42 @@ def tile_list_kvt_dl_scale_kernel(
                 weave_out_of_bank(q_woven[b], blk, q_banks[blk])
 
         wvd_q, kr_q = {}, {}
-        for a in range(PASSES):
-            wvd_q[a] = quantise_by_halves("wvd%d" % a, wvd_raw[a], AT_WVD_WOVEN[a])
+        for a, part in ((0, 0), (0, 1), (1, 0)):
+            wvd_q[a, part] = quantise_half("wvd%d" % a, wvd_raw[a], part, AT_WVD_WOVEN[a][part])
         qr_q = [quantise("qr%d" % b, q_woven[b], AT_QR_CODES[b]) for b in range(PASSES)]
         for b in range(PASSES):
             kr_q[b, 0] = quantise("kr%d0" % b, k_woven[b], AT_KR_CODES[0][b])
-        for b in range(PASSES):
-            kr_q[b, 1] = quantise("kr%d1" % b, k_late[b], AT_KR_CODES[1][b])
 
-        def change_pass(bank, a, nt, h, start):
-            codes, plane = wvd_q[a][nt // 2]
+        def change_pass(bank, a, nt, h, start, cols):
+            codes, plane = wvd_q[a, nt // 2]
             n_cols = slice(nt % 2 * P, (nt % 2 + 1) * P)
             nc.tensor.matmul_mx(
                 out=bank[:],
                 lhsT=codes[:, n_cols].bitcast(FP8X4),
                 lhsT_scale=plane[:, n_cols],
-                rhs=v_c[a, h][:].bitcast(FP8X4),
-                rhs_scale=v_s[a, h],
+                rhs=v_c[a, h][:, cols].bitcast(FP8X4),
+                rhs_scale=v_s[a, h][:, cols],
                 start=start,
                 stop=(a == PASSES - 1),
             )
 
-        def values(nt, h, pieces=1):
-            bank = new_bank([P, BANK])
+        def values(nt, h, c0=0, width=BANK):
+            bank = new_bank([P, width])
+            cols = slice(c0, c0 + width)
             begun = (nt, h) in partial
             if not begun:
-                base_pass(bank, 0, nt, h, True, False)
-            change_pass(bank, 0, nt, h, begun)
-            base_pass(bank, 1, nt, h, False, False)
-            change_pass(bank, 1, nt, h, False)
-            width = BANK // pieces
-            for piece in range(pieces):
-                cols = slice(piece * width, (piece + 1) * width)
-                res = outs.tile([P, width], F32, name="res")
-                if begun:
-                    nc.vector.tensor_tensor(res[:], bank[:, cols], partial[nt, h][:, cols], ADD)
-                else:
-                    nc.scalar.copy(res[:], bank[:, cols])
-                c0 = h * BANK + piece * width
-                nc.sync.dma_start(out_1[nt * P : (nt + 1) * P, c0 : c0 + width], res[:])
+                base_pass(bank[:], 0, nt, h, True, False)
+            change_pass(bank, 0, nt, h, begun, cols)
+            step = BANK if width == BANK else P
+            for c in range(0, width, step):
+                base_pass(bank[:, c : c + step], 1, nt, h, False, False, slice(c0 + c, c0 + c + step))
+            change_pass(bank, 1, nt, h, False, cols)
+            res = outs.tile([P, width], F32, name="res")
+            if begun:
+                nc.vector.tensor_tensor(res[:], bank[:], partial[nt, h][:, cols], ADD)
+            else:
+                nc.scalar.copy(res[:], bank[:])
+            nc.sync.dma_start(out_1[nt * P : (nt + 1) * P, h * BANK + c0 : h * BANK + c0 + width], res[:])
 
         def scores(mt, h, c0, width, on_vector):
             bank = new_bank([P, width])
@@ -355,10 +349,14 @@ def tile_list_kvt_dl_scale_kernel(
 
         values(0, 1)
         values(1, 1)
+        wvd_q[1, 1] = quantise_half("wvd1", wvd_raw[1], 1, AT_WVD_WOVEN[1][1])
+        for b in range(PASSES):
+            kr_q[b, 1] = quantise("kr%d1" % b, k_late[b], AT_KR_CODES[1][b])
         for mt in range(M // P):
             scores(mt, 0, 0, BANK, False)
         values(2, 1)
         for i in range(M // P):
             values(i, 0)
             scores(i, 1, 0, BANK, False)
-        values(3, 1, 2)
+        for part in range(2):
+            values(3, 1, part * BANK // 2, BANK // 2)

@@ -31,8 +31,8 @@ LINE = 4
 SCORE_SCALE = 0.03125
 ALIGN = 64
 PSUM_BANKS = 8
-RESULT_TILES = 17
-PARTIAL_TILES = 7
+RESULT_TILES = 18
+PARTIAL_TILES = 8
 
 KB = 1024
 AT_TABLE = (32 * KB, 0)
@@ -43,14 +43,15 @@ AT_WQ_S_RAW = 62 * KB
 AT_WQ_RAW = (33 * KB, 62 * KB)
 AT_WQ_ROWS = 58 * KB
 AT_WK0 = 58 * KB
+AT_WQ_PLANE = 37 * KB
 AT_LAST_WORDS = 17 * KB
 AT_X_RAW = (40 * KB, 25 * KB)
 AT_WV4_CODES = (None, 8 * KB)
-AT_WVD_WOVEN = ((None, None), (70 * KB, 92 * KB))
+AT_WVD_WOVEN = ((89 * KB, 94 * KB), (91 * KB, 96 * KB))
 AT_X_WOVEN = ((None, None), (80 * KB, 82 * KB))
-AT_WQ_CODES = (None, 79 * KB)
-AT_KR_CODES = ((None, 83 * KB), (88 * KB, 90 * KB))
-AT_Q_WOVEN = (86 * KB, 90 * KB)
+AT_WQ_CODES = (None, 77 * KB)
+AT_KR_CODES = ((62 * KB, 64 * KB), (85 * KB, 87 * KB))
+AT_Q_WOVEN = ((None, 90 * KB), (86 * KB, 95 * KB))
 AT_QR_CODES = (69 * KB, 71 * KB)
 AT_KR_WOVEN = (64 * KB, 92 * KB)
 
@@ -157,9 +158,7 @@ def tile_list_kvt_dl_scale_kernel(
         zero(nc.gpsimd, tab_s[64:128, :])
         planes = [tile("planes%d" % a, [P, J + R + N], U8) for a in range(PASSES)]
         zero(nc.vector, planes[0][:])
-        zero(nc.gpsimd, planes[1][:])
-        wq_plane = tile("wq_plane", [P, PASSES * R], U8)
-        zero(nc.gpsimd, wq_plane[:])
+        zero(nc.vector, planes[1][:])
 
         deal(rows[:, J : J + R], wk_s_raw[:], 2)
         picked_scales = tile("picked_s", [P, J], U8, AT_PICKED_SCALES)
@@ -184,6 +183,8 @@ def tile_list_kvt_dl_scale_kernel(
         x_raw = [load_f32("x", x, a, AT_X_RAW[a]) for a in range(PASSES)]
         wk_c = [tile("wk_c%d" % a, [P, 2 * R], U8) for a in range(PASSES)]
         deal(wk_c[0][:], wk_raw[0][:], 4)
+        wq_plane = tile("wq_plane", [P, PASSES * R], U8, AT_WQ_PLANE)
+        zero(nc.vector, wq_plane[:])
         wq_rows = tile("wq_rows", [BLOCKS, PASSES * R], U8, AT_WQ_ROWS)
         deal(wq_rows[:], wq_s_raw[:].rearrange("p a w -> p (a w)"), 2)
         spread_scale_rows(wq_plane, wq_rows, 0)
@@ -259,9 +260,10 @@ def tile_list_kvt_dl_scale_kernel(
 
         wq_c = [deal_wq(0)]
         x_q = []
-        for a in range(PASSES):
-            x_q.append([quantise_half("x%d" % a, x_raw[a], part, AT_X_WOVEN[a][part]) for part in range(2)])
+        x_q.append([quantise_half("x0", x_raw[0], part, AT_X_WOVEN[0][part]) for part in range(2)])
+        x_q.append([quantise_half("x1", x_raw[1], 0, AT_X_WOVEN[1][0])])
         wq_c.append(deal_wq(1))
+        x_q[1].append(quantise_half("x1", x_raw[1], 1, AT_X_WOVEN[1][1]))
 
         def query_passes(bank, a, b, blk):
             x_codes, x_plane = x_q[a][blk // 2]
@@ -278,22 +280,21 @@ def tile_list_kvt_dl_scale_kernel(
                     stop=(a == PASSES - 1 and t == PACK - 1),
                 )
 
-        q_woven = []
-        for b in range(PASSES):
-            q_woven.append(tile("q_woven%d" % b, [P, M, PACK], BF16, AT_Q_WOVEN[b]))
-            q_banks = [new_bank([P, PACK, P]) for blk in range(M // P)]
-            for blk in range(M // P):
-                query_passes(q_banks[blk], 0, b, blk)
-            for blk in range(M // P):
-                query_passes(q_banks[blk], 1, b, blk)
-                weave_out_of_bank(q_woven[b], blk, q_banks[blk])
+        qr_q, wvd_q, kr_q = {}, {}, {}
 
-        wvd_q, kr_q = {}, {}
-        for a, part in ((0, 0), (0, 1), (1, 0)):
-            wvd_q[a, part] = quantise_half("wvd%d" % a, wvd_raw[a], part, AT_WVD_WOVEN[a][part])
-        qr_q = [quantise("qr%d" % b, q_woven[b], AT_QR_CODES[b]) for b in range(PASSES)]
-        for b in range(PASSES):
-            kr_q[b, 0] = quantise("kr%d0" % b, k_woven[b], AT_KR_CODES[0][b])
+        def queries(b, part, grouped):
+            woven = tile("q_woven%d%d" % (b, part), [P, M // 2, PACK], BF16, AT_Q_WOVEN[b][part])
+            blks = (2 * part, 2 * part + 1)
+            banks = {blk: new_bank([P, PACK, P]) for blk in blks}
+            if grouped:
+                for blk in blks:
+                    query_passes(banks[blk], 0, b, blk)
+            for blk in blks:
+                if not grouped:
+                    query_passes(banks[blk], 0, b, blk)
+                query_passes(banks[blk], 1, b, blk)
+                weave_out_of_bank(woven, blk % 2, banks[blk])
+            qr_q[b, part] = quantise("qr%d%d" % (b, part), woven)
 
         def change_pass(bank, a, nt, h, start, cols):
             codes, plane = wvd_q[a, nt // 2]
@@ -329,12 +330,13 @@ def tile_list_kvt_dl_scale_kernel(
         def scores(mt, h, c0, width, on_vector):
             bank = new_bank([P, width])
             m_cols = slice(mt * P, (mt + 1) * P)
+            q_cols = slice(mt % 2 * P, (mt % 2 + 1) * P)
             j_cols = slice(c0, c0 + width)
             for b in range(PASSES):
                 nc.tensor.matmul_mx(
                     out=bank[:],
-                    lhsT=qr_q[b][0][:, m_cols].bitcast(FP8X4),
-                    lhsT_scale=qr_q[b][1][:, m_cols],
+                    lhsT=qr_q[b, mt // 2][0][:, q_cols].bitcast(FP8X4),
+                    lhsT_scale=qr_q[b, mt // 2][1][:, q_cols],
                     rhs=kr_q[b, h][0][:, j_cols].bitcast(FP8X4),
                     rhs_scale=kr_q[b, h][1][:, j_cols],
                     start=(b == 0),
@@ -347,16 +349,27 @@ def tile_list_kvt_dl_scale_kernel(
                 nc.scalar.activation(res[:], bank[:], COPY, scale=SCORE_SCALE)
             nc.sync.dma_start(out_0[m_cols, h * BANK + c0 : h * BANK + c0 + width], res[:])
 
-        values(0, 1)
-        values(1, 1)
-        wvd_q[1, 1] = quantise_half("wvd1", wvd_raw[1], 1, AT_WVD_WOVEN[1][1])
+        queries(0, 0, True)
+        queries(1, 0, False)
+        for h in range(HALVES):
+            for b in range(PASSES):
+                kr_q[b, h] = quantise("kr%d%d" % (b, h), (k_woven, k_late)[h][b], AT_KR_CODES[h][b])
         for b in range(PASSES):
-            kr_q[b, 1] = quantise("kr%d1" % b, k_late[b], AT_KR_CODES[1][b])
-        for mt in range(M // P):
-            scores(mt, 0, 0, BANK, False)
+            queries(b, 1, False)
+            for mt in range(2):
+                scores(mt, b, 0, BANK, False)
+        for a in range(PASSES):
+            wvd_q[a, 0] = quantise_half("wvd%d" % a, wvd_raw[a], 0, AT_WVD_WOVEN[a][0])
+        for h in range(HALVES):
+            for mt in range(2, 4):
+                scores(mt, h, 0, BANK, False)
+            values(0, h)
+        for a in range(PASSES):
+            wvd_q[a, 1] = quantise_half("wvd%d" % a, wvd_raw[a], 1, AT_WVD_WOVEN[a][1])
+        for h in range(HALVES):
+            values(1, h)
+        values(2, 0)
         values(2, 1)
-        for i in range(M // P):
-            values(i, 0)
-            scores(i, 1, 0, BANK, False)
-        for part in range(2):
-            values(3, 1, part * BANK // 2, BANK // 2)
+        values(3, 0)
+        for c0, width in ((0, 2 * P), (2 * P, P), (3 * P, P)):
+            values(3, 1, c0, width)

@@ -13,7 +13,6 @@ U16 = mybir.dt.uint16
 U8 = mybir.dt.uint8
 FP8X4 = mybir.dt.float8_e4m3fn_x4
 FP4X4 = mybir.dt.float4_e2m1fn_x4
-MULT = mybir.AluOpType.mult
 ADD = mybir.AluOpType.add
 COPY = mybir.ActivationFunctionType.Copy
 
@@ -31,29 +30,29 @@ LINE = 4
 SCORE_SCALE = 0.03125
 ALIGN = 64
 PSUM_BANKS = 8
+PARTS = 2
+PART = BANK // PARTS
+LAST_PIECES = ((0, 2 * P), (2 * P, P), (3 * P, P))
 RESULT_TILES = 18
-PARTIAL_TILES = 8
+KEY_BANKS_ON_VECTOR = ((0, 3), (1, 1))
 
 KB = 1024
-AT_TABLE = (32 * KB, 0)
 AT_PICKED_SCALES = 16 * KB - 512
+AT_TABLE = (32 * KB, 0)
+AT_WK_RAW = 16 * KB
+AT_LAST_WORDS = 17 * KB
 AT_WVD_RAW = (0, 9 * KB)
-AT_WK_RAW = (None, 16 * KB)
+AT_WV4_CODES = (None, 8 * KB)
+AT_X_RAW = (41 * KB, 25 * KB)
+AT_WQ_PLANE = 37 * KB
+AT_WQ_ROWS = 39 * KB
 AT_WQ_S_RAW = 62 * KB
 AT_WQ_RAW = (33 * KB, 62 * KB)
-AT_WQ_ROWS = 58 * KB
-AT_WK0 = 58 * KB
-AT_WQ_PLANE = 37 * KB
-AT_LAST_WORDS = 17 * KB
-AT_X_RAW = (40 * KB, 25 * KB)
-AT_WV4_CODES = (None, 8 * KB)
-AT_WVD_WOVEN = ((89 * KB, 94 * KB), (91 * KB, 96 * KB))
 AT_X_WOVEN = ((None, None), (80 * KB, 82 * KB))
 AT_WQ_CODES = (None, 77 * KB)
-AT_KR_CODES = ((62 * KB, 64 * KB), (85 * KB, 87 * KB))
 AT_Q_WOVEN = ((None, 90 * KB), (86 * KB, 95 * KB))
-AT_QR_CODES = (69 * KB, 71 * KB)
-AT_KR_WOVEN = (64 * KB, 92 * KB)
+AT_KR_CODES = ((62 * KB, 64 * KB), (85 * KB, 87 * KB))
+AT_WVD_WOVEN = ((89 * KB, 94 * KB), (91 * KB, 96 * KB))
 
 
 def tile_list_kvt_dl_scale_kernel(
@@ -85,9 +84,9 @@ def tile_list_kvt_dl_scale_kernel(
             nc.sync.dma_start(dst.bitcast(I32), src.rearrange("a g w -> (a g) w").bitcast(I32))
 
         def spread_scale_rows(plane, staged, first):
-            for s in range(QUADS):
+            for s in range(BLOCKS // QUADS):
                 nc.sync.dma_start(
-                    plane[s:P:32, :].bitcast(I32), staged[first + s : first + BLOCKS : QUADS, :].bitcast(I32)
+                    plane[s:P:32, :].bitcast(I32), staged[first + s : first + BLOCKS : BLOCKS // QUADS, :].bitcast(I32)
                 )
 
         def load_words(name, src, offset):
@@ -121,16 +120,13 @@ def tile_list_kvt_dl_scale_kernel(
             )
             return codes, scales
 
-        def weave_and_quantise(name, rows, woven, offset=None):
+        def quantise_part(name, raw, part, offset):
+            woven = tile("%s_woven%d" % (name, part), [P, PART, PACK], BF16, offset)
             nc.vector.tensor_copy(
-                woven[:].rearrange("p (c i) t -> p c t i", i=LINE), rows.rearrange("p t (c i) -> p c t i", i=LINE)
+                woven[:].rearrange("p (c i) t -> p c t i", i=LINE),
+                raw[:, :, part * PART : (part + 1) * PART].rearrange("p t (c i) -> p c t i", i=LINE),
             )
-            return quantise(name, woven, offset)
-
-        def quantise_half(name, raw, part, offset_woven):
-            woven = tile("%s_woven%d" % (name, part), [P, BANK // 2, PACK], BF16, offset_woven)
-            cols = slice(part * BANK // 2, (part + 1) * BANK // 2)
-            return weave_and_quantise("%s_%d" % (name, part), raw[:, :, cols], woven)
+            return quantise("%s_%d" % (name, part), woven)
 
         def weave_out_of_bank(woven, blk, bank, on_vector=False):
             copy = nc.vector.tensor_copy if on_vector else nc.scalar.copy
@@ -152,21 +148,22 @@ def tile_list_kvt_dl_scale_kernel(
         nc.sync.dma_start(wq_s_raw[:].bitcast(I32), wq_scales.rearrange("a g w -> g a w").bitcast(I32))
         tab_w = [load_table(0)]
         wv4_c = [load_wv4(0)]
-        wk_raw = [load_words("wk_raw0", wk_words[0].bitcast(I32), AT_WK0)]
 
         zero(nc.vector, tab_s[32:64, :])
         zero(nc.gpsimd, tab_s[64:128, :])
         planes = [tile("planes%d" % a, [P, J + R + N], U8) for a in range(PASSES)]
-        zero(nc.vector, planes[0][:])
-        zero(nc.vector, planes[1][:])
+        for a in range(PASSES):
+            zero(nc.vector, planes[a][:])
 
         deal(rows[:, J : J + R], wk_s_raw[:], 2)
         picked_scales = tile("picked_s", [P, J], U8, AT_PICKED_SCALES)
         nc.vector.tensor_copy(picked_scales[:], tab_s[:].indirect(offsets[:]))
         nc.vector.tensor_copy(rows[:, :J].bitcast(I32), picked_scales[0:SCALE_ROWS, :].bitcast(I32))
         spread_scale_rows(planes[0], rows, 0)
+        wk_raw = tile("wk_raw", [P, PASSES, R // 2], I32, AT_WK_RAW)
+        nc.sync.dma_start(wk_raw[:, 0], wk_words[0].bitcast(I32))
         tab_w.append(load_table(1))
-        wk_raw.append(load_words("wk_raw1", wk_words[1].bitcast(I32), AT_WK_RAW[1]))
+        nc.sync.dma_start(wk_raw[:, 1], wk_words[1].bitcast(I32))
         spread_scale_rows(planes[1], rows, BLOCKS)
 
         v_c, v_s = {}, {}
@@ -182,7 +179,7 @@ def tile_list_kvt_dl_scale_kernel(
         wq_raw = [load_wq(0)]
         x_raw = [load_f32("x", x, a, AT_X_RAW[a]) for a in range(PASSES)]
         wk_c = [tile("wk_c%d" % a, [P, 2 * R], U8) for a in range(PASSES)]
-        deal(wk_c[0][:], wk_raw[0][:], 4)
+        deal(wk_c[0][:], wk_raw[:, 0], 4)
         wq_plane = tile("wq_plane", [P, PASSES * R], U8, AT_WQ_PLANE)
         zero(nc.vector, wq_plane[:])
         wq_rows = tile("wq_rows", [BLOCKS, PASSES * R], U8, AT_WQ_ROWS)
@@ -190,7 +187,7 @@ def tile_list_kvt_dl_scale_kernel(
         spread_scale_rows(wq_plane, wq_rows, 0)
         wq_raw.append(load_wq(1))
 
-        def base_pass(out, a, nt, h, start, stop, cols=slice(0, BANK)):
+        def base_pass(out, a, nt, h, cols, start, stop):
             nc.tensor.matmul_mx(
                 out=out,
                 lhsT=wv4_c[a][:, 2 * nt * P : 2 * (nt + 1) * P].bitcast(FP4X4),
@@ -201,57 +198,50 @@ def tile_list_kvt_dl_scale_kernel(
                 stop=stop,
             )
 
-        value_tiles = [(nt, 0) for nt in range(N // P)] + [(nt, 1) for nt in reversed(range(N // P))]
         partial = {}
-        for nt, h in value_tiles[:PARTIAL_TILES]:
+        for nt, h in [(nt, 0) for nt in range(N // P)] + [(nt, 1) for nt in reversed(range(N // P))]:
             bank = new_bank([P, BANK])
-            base_pass(bank[:], 0, nt, h, True, True)
+            base_pass(bank[:], 0, nt, h, slice(0, BANK), True, True)
             partial[nt, h] = tile("partial%d%d" % (nt, h), [P, BANK], F32)
             nc.scalar.copy(partial[nt, h][:], bank[:])
 
-        def key_pass(out, a, b, t, h, cols, start, stop):
-            col = (b * PACK + t) * P
-            nc.tensor.matmul_mx(
-                out=out,
-                lhsT=wk_c[a][:, 2 * col : 2 * (col + P)].bitcast(FP4X4),
-                lhsT_scale=planes[a][:, J + col : J + col + P],
-                rhs=v_c[a, h][:, cols].bitcast(FP8X4),
-                rhs_scale=v_s[a, h][:, cols],
-                start=start,
-                stop=stop,
-            )
+        def key_passes(bank, a, b, h, blk):
+            cols = slice(blk * P, (blk + 1) * P)
+            for t in range(PACK):
+                col = (b * PACK + t) * P
+                nc.tensor.matmul_mx(
+                    out=bank[:, t, :],
+                    lhsT=wk_c[a][:, 2 * col : 2 * (col + P)].bitcast(FP4X4),
+                    lhsT_scale=planes[a][:, J + col : J + col + P],
+                    rhs=v_c[a, h][:, cols].bitcast(FP8X4),
+                    rhs_scale=v_s[a, h][:, cols],
+                    start=(a == 0 and t == 0),
+                    stop=(a == PASSES - 1 and t == PACK - 1),
+                )
 
         k_banks = {}
-
-        def narrow_key_passes(a, b, blk, h=0):
-            for t in range(PACK):
-                first, last = a == 0 and t == 0, a == PASSES - 1 and t == PACK - 1
-                key_pass(k_banks[b, blk][:, t, :], a, b, t, h, slice(blk * P, (blk + 1) * P), first, last)
-
         for b in range(PASSES):
             for blk in range(BANK // P):
                 k_banks[b, blk] = new_bank([P, PACK, P])
-                narrow_key_passes(0, b, blk)
+                key_passes(k_banks[b, blk], 0, b, 0, blk)
         gather(1, 0)
-        deal(wk_c[1][:], wk_raw[1][:], 4)
+        deal(wk_c[1][:], wk_raw[:, 1], 4)
         gather(1, 1, AT_LAST_WORDS)
         wvd_raw = [load_f32("wvd", wvd, a, AT_WVD_RAW[a]) for a in range(PASSES)]
         wv4_c.append(load_wv4(1))
-        k_woven = []
+        k_woven = {}
         for b in range(PASSES):
-            k_woven.append(tile("k_woven%d" % b, [P, BANK, PACK], BF16))
+            k_woven[b, 0] = tile("k_woven%d0" % b, [P, BANK, PACK], BF16)
             for blk in range(BANK // P):
-                narrow_key_passes(1, b, blk)
-                weave_out_of_bank(k_woven[b], blk, k_banks[b, blk], (b, blk) in ((0, 3), (1, 1)))
-
-        k_late = []
+                key_passes(k_banks[b, blk], 1, b, 0, blk)
+                weave_out_of_bank(k_woven[b, 0], blk, k_banks[b, blk], (b, blk) in KEY_BANKS_ON_VECTOR)
         for b in range(PASSES):
-            k_late.append(tile("k_late%d" % b, [P, BANK, PACK], BF16))
+            k_woven[b, 1] = tile("k_woven%d1" % b, [P, BANK, PACK], BF16)
             for blk in range(BANK // P):
-                k_banks[b, blk] = new_bank([P, PACK, P])
+                bank = new_bank([P, PACK, P])
                 for a in range(PASSES):
-                    narrow_key_passes(a, b, blk, 1)
-                weave_out_of_bank(k_late[b], blk, k_banks[b, blk])
+                    key_passes(bank, a, b, 1, blk)
+                weave_out_of_bank(k_woven[b, 1], blk, bank)
 
         def deal_wq(b):
             codes = tile("wq_c%d" % b, [P, PASSES, K_PASS], U32, AT_WQ_CODES[b])
@@ -259,11 +249,10 @@ def tile_list_kvt_dl_scale_kernel(
             return codes
 
         wq_c = [deal_wq(0)]
-        x_q = []
-        x_q.append([quantise_half("x0", x_raw[0], part, AT_X_WOVEN[0][part]) for part in range(2)])
-        x_q.append([quantise_half("x1", x_raw[1], 0, AT_X_WOVEN[1][0])])
+        x_q = [[quantise_part("x0", x_raw[0], part, AT_X_WOVEN[0][part]) for part in range(PARTS)]]
+        x_q.append([quantise_part("x1", x_raw[1], 0, AT_X_WOVEN[1][0])])
         wq_c.append(deal_wq(1))
-        x_q[1].append(quantise_half("x1", x_raw[1], 1, AT_X_WOVEN[1][1]))
+        x_q[1].append(quantise_part("x1", x_raw[1], 1, AT_X_WOVEN[1][1]))
 
         def query_passes(bank, a, b, blk):
             x_codes, x_plane = x_q[a][blk // 2]
@@ -282,21 +271,38 @@ def tile_list_kvt_dl_scale_kernel(
 
         qr_q, wvd_q, kr_q = {}, {}, {}
 
-        def queries(b, part, grouped):
-            woven = tile("q_woven%d%d" % (b, part), [P, M // 2, PACK], BF16, AT_Q_WOVEN[b][part])
+        def queries(b, part, pass_0_first):
+            woven = tile("q_woven%d%d" % (b, part), [P, PART, PACK], BF16, AT_Q_WOVEN[b][part])
             blks = (2 * part, 2 * part + 1)
             banks = {blk: new_bank([P, PACK, P]) for blk in blks}
-            if grouped:
+            if pass_0_first:
                 for blk in blks:
                     query_passes(banks[blk], 0, b, blk)
             for blk in blks:
-                if not grouped:
+                if not pass_0_first:
                     query_passes(banks[blk], 0, b, blk)
                 query_passes(banks[blk], 1, b, blk)
                 weave_out_of_bank(woven, blk % 2, banks[blk])
             qr_q[b, part] = quantise("qr%d%d" % (b, part), woven)
 
-        def change_pass(bank, a, nt, h, start, cols):
+        def scores(mt, h):
+            bank = new_bank([P, BANK])
+            q_cols = slice(mt % 2 * P, (mt % 2 + 1) * P)
+            for b in range(PASSES):
+                nc.tensor.matmul_mx(
+                    out=bank[:],
+                    lhsT=qr_q[b, mt // 2][0][:, q_cols].bitcast(FP8X4),
+                    lhsT_scale=qr_q[b, mt // 2][1][:, q_cols],
+                    rhs=kr_q[b, h][0][:].bitcast(FP8X4),
+                    rhs_scale=kr_q[b, h][1][:],
+                    start=(b == 0),
+                    stop=(b == PASSES - 1),
+                )
+            res = outs.tile([P, BANK], F32, name="res")
+            nc.scalar.activation(res[:], bank[:], COPY, scale=SCORE_SCALE)
+            nc.sync.dma_start(out_0[mt * P : (mt + 1) * P, h * BANK : (h + 1) * BANK], res[:])
+
+        def change_pass(bank, a, nt, h, cols):
             codes, plane = wvd_q[a, nt // 2]
             n_cols = slice(nt % 2 * P, (nt % 2 + 1) * P)
             nc.tensor.matmul_mx(
@@ -305,71 +311,43 @@ def tile_list_kvt_dl_scale_kernel(
                 lhsT_scale=plane[:, n_cols],
                 rhs=v_c[a, h][:, cols].bitcast(FP8X4),
                 rhs_scale=v_s[a, h][:, cols],
-                start=start,
+                start=(a == 0),
                 stop=(a == PASSES - 1),
             )
 
         def values(nt, h, c0=0, width=BANK):
             bank = new_bank([P, width])
             cols = slice(c0, c0 + width)
-            begun = (nt, h) in partial
-            if not begun:
-                base_pass(bank[:], 0, nt, h, True, False)
-            change_pass(bank, 0, nt, h, begun, cols)
+            change_pass(bank, 0, nt, h, cols)
             step = BANK if width == BANK else P
             for c in range(0, width, step):
-                base_pass(bank[:, c : c + step], 1, nt, h, False, False, slice(c0 + c, c0 + c + step))
-            change_pass(bank, 1, nt, h, False, cols)
+                base_pass(bank[:, c : c + step], 1, nt, h, slice(c0 + c, c0 + c + step), False, False)
+            change_pass(bank, 1, nt, h, cols)
             res = outs.tile([P, width], F32, name="res")
-            if begun:
-                nc.vector.tensor_tensor(res[:], bank[:], partial[nt, h][:, cols], ADD)
-            else:
-                nc.scalar.copy(res[:], bank[:])
+            nc.vector.tensor_tensor(res[:], bank[:], partial[nt, h][:, cols], ADD)
             nc.sync.dma_start(out_1[nt * P : (nt + 1) * P, h * BANK + c0 : h * BANK + c0 + width], res[:])
-
-        def scores(mt, h, c0, width, on_vector):
-            bank = new_bank([P, width])
-            m_cols = slice(mt * P, (mt + 1) * P)
-            q_cols = slice(mt % 2 * P, (mt % 2 + 1) * P)
-            j_cols = slice(c0, c0 + width)
-            for b in range(PASSES):
-                nc.tensor.matmul_mx(
-                    out=bank[:],
-                    lhsT=qr_q[b, mt // 2][0][:, q_cols].bitcast(FP8X4),
-                    lhsT_scale=qr_q[b, mt // 2][1][:, q_cols],
-                    rhs=kr_q[b, h][0][:, j_cols].bitcast(FP8X4),
-                    rhs_scale=kr_q[b, h][1][:, j_cols],
-                    start=(b == 0),
-                    stop=(b == PASSES - 1),
-                )
-            res = outs.tile([P, width], F32, name="res")
-            if on_vector:
-                nc.vector.tensor_scalar(res[:], bank[:], SCORE_SCALE, None, MULT)
-            else:
-                nc.scalar.activation(res[:], bank[:], COPY, scale=SCORE_SCALE)
-            nc.sync.dma_start(out_0[m_cols, h * BANK + c0 : h * BANK + c0 + width], res[:])
 
         queries(0, 0, True)
         queries(1, 0, False)
         for h in range(HALVES):
             for b in range(PASSES):
-                kr_q[b, h] = quantise("kr%d%d" % (b, h), (k_woven, k_late)[h][b], AT_KR_CODES[h][b])
+                kr_q[b, h] = quantise("kr%d%d" % (b, h), k_woven[b, h], AT_KR_CODES[h][b])
         for b in range(PASSES):
             queries(b, 1, False)
+
+        for h in range(HALVES):
             for mt in range(2):
-                scores(mt, b, 0, BANK, False)
+                scores(mt, h)
         for a in range(PASSES):
-            wvd_q[a, 0] = quantise_half("wvd%d" % a, wvd_raw[a], 0, AT_WVD_WOVEN[a][0])
+            wvd_q[a, 0] = quantise_part("wvd%d" % a, wvd_raw[a], 0, AT_WVD_WOVEN[a][0])
         for h in range(HALVES):
             for mt in range(2, 4):
-                scores(mt, h, 0, BANK, False)
+                scores(mt, h)
             values(0, h)
         for a in range(PASSES):
-            wvd_q[a, 1] = quantise_half("wvd%d" % a, wvd_raw[a], 1, AT_WVD_WOVEN[a][1])
-        for h in range(HALVES):
-            values(1, h)
-        values(2, 0)
-        values(2, 1)
-        values(3, 0)
-        for c0, width in ((0, 2 * P), (2 * P, P), (3 * P, P)):
-            values(3, 1, c0, width)
+            wvd_q[a, 1] = quantise_part("wvd%d" % a, wvd_raw[a], 1, AT_WVD_WOVEN[a][1])
+        late_tiles = [(nt, h) for nt in range(1, N // P) for h in range(HALVES)]
+        for nt, h in late_tiles[:-1]:
+            values(nt, h)
+        for c0, width in LAST_PIECES:
+            values(*late_tiles[-1], c0, width)

@@ -32,8 +32,8 @@ ALIGN = 64
 PSUM_BANKS = 8
 PARTS = 2
 PART = BANK // PARTS
-LAST_PIECES = ((0, 2 * P), (2 * P, P), (3 * P, P))
-RESULT_TILES = 18
+LAST_PIECES = (((0, 2 * P), (2 * P, 2 * P)), ((0, 2 * P), (2 * P, P), (3 * P, P)))
+RESULT_TILES = 19
 KEY_BANKS_ON_VECTOR = ((0, 3), (1, 1))
 
 KB = 1024
@@ -319,9 +319,7 @@ def tile_list_kvt_dl_scale_kernel(
             bank = new_bank([P, width])
             cols = slice(c0, c0 + width)
             change_pass(bank, 0, nt, h, cols)
-            step = BANK if width == BANK else P
-            for c in range(0, width, step):
-                base_pass(bank[:, c : c + step], 1, nt, h, slice(c0 + c, c0 + c + step), False, False)
+            base_pass(bank[:], 1, nt, h, cols, False, False)
             change_pass(bank, 1, nt, h, cols)
             res = outs.tile([P, width], F32, name="res")
             nc.vector.tensor_tensor(res[:], bank[:], partial[nt, h][:, cols], ADD)
@@ -347,7 +345,8 @@ def tile_list_kvt_dl_scale_kernel(
         for a in range(PASSES):
             wvd_q[a, 1] = quantise_part("wvd%d" % a, wvd_raw[a], 1, AT_WVD_WOVEN[a][1])
         late_tiles = [(nt, h) for nt in range(1, N // P) for h in range(HALVES)]
-        for nt, h in late_tiles[:-1]:
+        for nt, h in late_tiles[: -len(LAST_PIECES)]:
             values(nt, h)
-        for c0, width in LAST_PIECES:
-            values(*late_tiles[-1], c0, width)
+        for (nt, h), pieces in zip(late_tiles[-len(LAST_PIECES) :], LAST_PIECES):
+            for c0, width in pieces:
+                values(nt, h, c0, width)

@@ -25,6 +25,7 @@ HALVES = J // BANK
 QUADS = 4
 BLOCKS = 16
 SCALE_ROWS = PASSES * BLOCKS
+STAGED = P - SCALE_ROWS
 LIST_ROWS = 16
 LINE = 4
 SCORE_SCALE = 0.03125
@@ -47,6 +48,8 @@ AT_X_RAW = (41 * KB, 25 * KB)
 AT_WQ_PLANE = 37 * KB
 AT_WQ_ROWS = 39 * KB
 AT_WQ_S_RAW = 62 * KB
+AT_WK_S_RAW = 100 * KB
+AT_PLANES = (None, 100 * KB)
 AT_WQ_RAW = (33 * KB, 62 * KB)
 AT_X_WOVEN = ((None, None), (80 * KB, 82 * KB))
 AT_WQ_CODES = (None, 77 * KB)
@@ -106,10 +109,10 @@ def tile_list_kvt_dl_scale_kernel(
             nc.sync.dma_start(raw[:], src[a * K_PASS : (a + 1) * K_PASS, :].rearrange("(p t) w -> p t w", t=PACK))
             return raw
 
-        def deal(dst, src, run):
-            nc.vector.tensor_copy(
-                dst.bitcast(I32).rearrange("p (c t g w) -> p c t g w", t=PACK, g=BLOCKS, w=run),
-                src.bitcast(I32).rearrange("p (c g t w) -> p c t g w", t=PACK, g=BLOCKS, w=run),
+        def deal(dst, src, run, copy=nc.vector.tensor_copy, word=I32):
+            copy(
+                dst.bitcast(word).rearrange("p (c t g w) -> p c t g w", t=PACK, g=BLOCKS, w=run),
+                src.bitcast(word).rearrange("p (c g t w) -> p c t g w", t=PACK, g=BLOCKS, w=run),
             )
 
         def quantise(name, woven, offset=None):
@@ -138,33 +141,33 @@ def tile_list_kvt_dl_scale_kernel(
             return codes
 
         tab_s = tile("tab_s", [P, T], U8)
-        load_scale_rows(tab_s[0:SCALE_ROWS, :], tab_scales)
+        load_scale_rows(tab_s[STAGED:, :], tab_scales)
         nc.sync.dma_start(offsets[:], offs)
-        wk_s_raw = tile("wk_s_raw", [SCALE_ROWS, R], U8)
-        load_scale_rows(wk_s_raw[:], wk_scales)
-        rows = tile("rows", [SCALE_ROWS, J + R + N], U8)
-        load_scale_rows(rows[:, J + R :], wv4_scales)
+        wk_s_raw = tile("wk_s_raw", [P, R], U8, AT_WK_S_RAW)
+        load_scale_rows(wk_s_raw[STAGED:, :], wk_scales)
+        rows = tile("rows", [P, J + R + N], U8)
+        load_scale_rows(rows[STAGED:, J + R :], wv4_scales)
         wq_s_raw = tile("wq_s_raw", [BLOCKS, PASSES, R], U8, AT_WQ_S_RAW)
         nc.sync.dma_start(wq_s_raw[:].bitcast(I32), wq_scales.rearrange("a g w -> g a w").bitcast(I32))
         tab_w = [load_table(0)]
         wv4_c = [load_wv4(0)]
 
-        zero(nc.vector, tab_s[32:64, :])
-        zero(nc.gpsimd, tab_s[64:128, :])
-        planes = [tile("planes%d" % a, [P, J + R + N], U8) for a in range(PASSES)]
-        for a in range(PASSES):
-            zero(nc.vector, planes[a][:])
+        zero(nc.vector, tab_s[:STAGED, :])
+        planes = [tile("planes0", [P, J + R + N], U8, AT_PLANES[0])]
+        zero(nc.vector, planes[0][:])
 
-        deal(rows[:, J : J + R], wk_s_raw[:], 2)
+        deal(rows[STAGED:, J : J + R], wk_s_raw[STAGED:, :], 2, nc.scalar.copy, U32)
         picked_scales = tile("picked_s", [P, J], U8, AT_PICKED_SCALES)
         nc.vector.tensor_copy(picked_scales[:], tab_s[:].indirect(offsets[:]))
-        nc.vector.tensor_copy(rows[:, :J].bitcast(I32), picked_scales[0:SCALE_ROWS, :].bitcast(I32))
-        spread_scale_rows(planes[0], rows, 0)
+        nc.vector.tensor_copy(rows[STAGED:, :J].bitcast(I32), picked_scales[STAGED:, :].bitcast(I32))
+        spread_scale_rows(planes[0], rows, STAGED)
+        planes.append(tile("planes1", [P, J + R + N], U8, AT_PLANES[1]))
+        zero(nc.vector, planes[1][:])
         wk_raw = tile("wk_raw", [P, PASSES, R // 2], I32, AT_WK_RAW)
         nc.sync.dma_start(wk_raw[:, 0], wk_words[0].bitcast(I32))
         tab_w.append(load_table(1))
         nc.sync.dma_start(wk_raw[:, 1], wk_words[1].bitcast(I32))
-        spread_scale_rows(planes[1], rows, BLOCKS)
+        spread_scale_rows(planes[1], rows, STAGED + BLOCKS)
 
         v_c, v_s = {}, {}
 

@@ -48,8 +48,6 @@ AT_X_RAW = (41 * KB, 25 * KB)
 AT_WQ_PLANE = 37 * KB
 AT_WQ_ROWS = 39 * KB
 AT_WQ_S_RAW = 62 * KB
-AT_WK_S_RAW = 100 * KB
-AT_PLANES = (None, 100 * KB)
 AT_WQ_RAW = (33 * KB, 62 * KB)
 AT_X_WOVEN = ((None, None), (80 * KB, 82 * KB))
 AT_WQ_CODES = (None, 77 * KB)
@@ -143,7 +141,7 @@ def tile_list_kvt_dl_scale_kernel(
         tab_s = tile("tab_s", [P, T], U8)
         load_scale_rows(tab_s[STAGED:, :], tab_scales)
         nc.sync.dma_start(offsets[:], offs)
-        wk_s_raw = tile("wk_s_raw", [P, R], U8, AT_WK_S_RAW)
+        wk_s_raw = tile("wk_s_raw", [P, R], U8)
         load_scale_rows(wk_s_raw[STAGED:, :], wk_scales)
         rows = tile("rows", [P, J + R + N], U8)
         load_scale_rows(rows[STAGED:, J + R :], wv4_scales)
@@ -153,16 +151,15 @@ def tile_list_kvt_dl_scale_kernel(
         wv4_c = [load_wv4(0)]
 
         zero(nc.vector, tab_s[:STAGED, :])
-        planes = [tile("planes0", [P, J + R + N], U8, AT_PLANES[0])]
-        zero(nc.vector, planes[0][:])
+        planes = [tile("planes%d" % a, [P, J + R + N], U8) for a in range(PASSES)]
+        for a in range(PASSES):
+            zero(nc.vector, planes[a][:])
 
         deal(rows[STAGED:, J : J + R], wk_s_raw[STAGED:, :], 2, nc.scalar.copy, U32)
         picked_scales = tile("picked_s", [P, J], U8, AT_PICKED_SCALES)
         nc.vector.tensor_copy(picked_scales[:], tab_s[:].indirect(offsets[:]))
         nc.vector.tensor_copy(rows[STAGED:, :J].bitcast(I32), picked_scales[STAGED:, :].bitcast(I32))
         spread_scale_rows(planes[0], rows, STAGED)
-        planes.append(tile("planes1", [P, J + R + N], U8, AT_PLANES[1]))
-        zero(nc.vector, planes[1][:])
         wk_raw = tile("wk_raw", [P, PASSES, R // 2], I32, AT_WK_RAW)
         nc.sync.dma_start(wk_raw[:, 0], wk_words[0].bitcast(I32))
         tab_w.append(load_table(1))

@@ -42,8 +42,8 @@ AT_PICKED_SCALES = 16 * KB - 512
 AT_TABLE = (32 * KB, 0)
 AT_WK_RAW = 16 * KB
 AT_LAST_WORDS = 17 * KB
-AT_WVD_RAW = (0, 9 * KB)
-AT_WV4_CODES = (None, 8 * KB)
+AT_WVD_RAW = 1 * KB
+AT_WV4_CODES = (None, 0)
 AT_X_RAW = (41 * KB, 25 * KB)
 AT_WQ_PLANE = 37 * KB
 AT_WQ_ROWS = 39 * KB
@@ -163,8 +163,10 @@ def tile_list_kvt_dl_scale_kernel(
         wk_raw = tile("wk_raw", [P, PASSES, R // 2], I32, AT_WK_RAW)
         nc.sync.dma_start(wk_raw[:, 0], wk_words[0].bitcast(I32))
         tab_w.append(load_table(1))
-        nc.sync.dma_start(wk_raw[:, 1], wk_words[1].bitcast(I32))
+        half = R // 4
+        nc.sync.dma_start(wk_raw[:, 1, :half], wk_words[1].bitcast(I32)[:, :half])
         spread_scale_rows(planes[1], rows, STAGED + BLOCKS)
+        nc.sync.dma_start(wk_raw[:, 1, half:], wk_words[1].bitcast(I32)[:, half:])
 
         v_c, v_s = {}, {}
 
@@ -225,9 +227,12 @@ def tile_list_kvt_dl_scale_kernel(
                 k_banks[b, blk] = new_bank([P, PACK, P])
                 key_passes(k_banks[b, blk], 0, b, 0, blk)
         gather(1, 0)
-        deal(wk_c[1][:], wk_raw[:, 1], 4)
+        deal(wk_c[1][:, :R], wk_raw[:, 1, :half], 4)
+        deal(wk_c[1][:, R:], wk_raw[:, 1, half:], 4)
         gather(1, 1, AT_LAST_WORDS)
-        wvd_raw = [load_f32("wvd", wvd, a, AT_WVD_RAW[a]) for a in range(PASSES)]
+        wvd_rows = tile("wvd_raw", [P, PASSES, PACK * N], F32, AT_WVD_RAW)
+        nc.sync.dma_start(wvd_rows[:], wvd.rearrange("(a p t) w -> p a (t w)", a=PASSES, t=PACK))
+        wvd_raw = [wvd_rows[:, a].rearrange("p (t w) -> p t w", t=PACK) for a in range(PASSES)]
         wv4_c.append(load_wv4(1))
         k_woven = {}
         for b in range(PASSES):

from contextlib import ExitStack

import concourse.mybir as mybir

K, R, M, N, T, J = 1024, 1024, 512, 512, 4096, 1024
FLOPS = 2 * K * R * M + 2 * K * R * J + 2 * R * M * J + 4 * K * N * J

F32 = mybir.dt.float32
BF16 = mybir.dt.bfloat16
I32 = mybir.dt.int32
U32 = mybir.dt.uint32
U16 = mybir.dt.uint16
U8 = mybir.dt.uint8
FP8X4 = mybir.dt.float8_e4m3fn_x4
FP4X4 = mybir.dt.float4_e2m1fn_x4
ADD = mybir.AluOpType.add
COPY = mybir.ActivationFunctionType.Copy

P = 128
PACK = 4
PASSES = 2
K_PASS = P * PACK
BANK = 512
HALVES = J // BANK
QUADS = 4
BLOCKS = 16
SCALE_ROWS = PASSES * BLOCKS
STAGED = P - SCALE_ROWS
LIST_ROWS = 16
LINE = 4
SCORE_SCALE = 0.03125
ALIGN = 64
PSUM_BANKS = 8
PARTS = 2
PART = BANK // PARTS
LAST_PIECES = (((0, 2 * P), (2 * P, 2 * P)), ((0, 2 * P), (2 * P, P), (3 * P, P)))
RESULT_TILES = 19
KEY_BANKS_ON_VECTOR = ((0, 3), (1, 1))

KB = 1024
AT_PICKED_SCALES = 16 * KB - 512
AT_TABLE = (32 * KB, 0)
AT_WK_RAW = 16 * KB
AT_LAST_WORDS = 17 * KB
AT_WVD_RAW = 1 * KB
AT_WV4_CODES = (None, 0)
AT_X_RAW = (41 * KB, 25 * KB)
AT_WQ_PLANE = 37 * KB
AT_WQ_ROWS = 39 * KB
AT_WQ_S_RAW = 62 * KB
AT_WQ_RAW = (33 * KB, 62 * KB)
AT_X_WOVEN = ((None, None), (80 * KB, 82 * KB))
AT_WQ_CODES = (None, 77 * KB)
AT_Q_WOVEN = ((None, 90 * KB), (86 * KB, 95 * KB))
AT_KR_CODES = ((62 * KB, 64 * KB), (85 * KB, 87 * KB))
AT_WVD_WOVEN = ((89 * KB, 94 * KB), (91 * KB, 96 * KB))


def tile_list_kvt_dl_scale_kernel(
    tc, tab_words, tab_scales, x, wq_words, wq_scales, wk_words, wk_scales, wv4_words, wv4_scales, wvd, offs,
    out_0, out_1,
):
    nc = tc.nc
    with ExitStack() as ctx:
        held = ctx.enter_context(tc.tile_pool(name="held", bufs=1))
        keep = ctx.enter_context(tc.tile_pool(name="keep", bufs=1))
        placed = ctx.enter_context(tc.tile_pool(name="placed", bufs=1))
        outs = ctx.enter_context(tc.tile_pool(name="outs", bufs=RESULT_TILES))
        psum = ctx.enter_context(tc.psum_pool(name="psum", bufs=PSUM_BANKS))

        offsets = held.tile([P, J // LIST_ROWS], U16, name="offsets")

        def tile(name, shape, dtype, offset=None):
            if offset is None:
                return keep.tile(shape, dtype, name=name, tag=name, align_bytes=ALIGN)
            return placed.tile(shape, dtype, name=name, tag=name, align_bytes=ALIGN, offset=offset)

        def new_bank(shape):
            return psum.tile(shape, F32, name="bank")

        def zero(engine, region):
            engine.memset(region.bitcast(I32), 0)

        def load_scale_rows(dst, src):
            nc.sync.dma_start(dst.bitcast(I32), src.rearrange("a g w -> (a g) w").bitcast(I32))

        def spread_scale_rows(plane, staged, first):
            for s in range(BLOCKS // QUADS):
                nc.sync.dma_start(
                    plane[s:P:32, :].bitcast(I32), staged[first + s : first + BLOCKS : BLOCKS // QUADS, :].bitcast(I32)
                )

        def load_words(name, src, offset):
            words = tile(name, [P] + list(src.shape[1:]), I32, offset)
            nc.sync.dma_start(words[:], src)
            return words

        def load_table(a):
            return load_words("tab_w%d" % a, tab_words[a].rearrange("p t i -> p (t i)").bitcast(I32), AT_TABLE[a])

        def load_wq(b):
            src = wq_words[:, :, b * K_PASS : (b + 1) * K_PASS, :]
            return load_words("wq_raw%d" % b, src.rearrange("a p r i -> p a (r i)").bitcast(I32), AT_WQ_RAW[b])

        def load_f32(name, src, a, offset):
            raw = tile("%s_raw%d" % (name, a), [P, PACK, BANK], F32, offset)
            nc.sync.dma_start(raw[:], src[a * K_PASS : (a + 1) * K_PASS, :].rearrange("(p t) w -> p t w", t=PACK))
            return raw

        def deal(dst, src, run, copy=nc.vector.tensor_copy, word=I32):
            copy(
                dst.bitcast(word).rearrange("p (c t g w) -> p c t g w", t=PACK, g=BLOCKS, w=run),
                src.bitcast(word).rearrange("p (c g t w) -> p c t g w", t=PACK, g=BLOCKS, w=run),
            )

        def quantise(name, woven, offset=None):
            codes = tile(name + "_c", [P, woven.shape[1]], U32, offset)
            scales = tile(name + "_s", [P, woven.shape[1]], U8)
            nc.vector.quantize_mx(
                out=codes[:].bitcast(FP8X4), scales=scales[:], in_=woven[:].rearrange("p j t -> p (j t)")
            )
            return codes, scales

        def quantise_part(name, raw, part, offset):
            woven = tile("%s_woven%d" % (name, part), [P, PART, PACK], BF16, offset)
            nc.vector.tensor_copy(
                woven[:].rearrange("p (c i) t -> p c t i", i=LINE),
                raw[:, :, part * PART : (part + 1) * PART].rearrange("p t (c i) -> p c t i", i=LINE),
            )
            return quantise("%s_%d" % (name, part), woven)

        def weave_out_of_bank(woven, blk, bank, on_vector=False):
            copy = nc.vector.tensor_copy if on_vector else nc.scalar.copy
            copy(woven[:, blk * P : (blk + 1) * P, :], bank[:].rearrange("p t j -> p j t"))

        def load_wv4(a):
            codes = tile("wv4_c%d" % a, [P, 2 * N], U8, AT_WV4_CODES[a])
            nc.sync.dma_start(codes[:].bitcast(I32), wv4_words[a].bitcast(I32))
            return codes

        tab_s = tile("tab_s", [P, T], U8)
        load_scale_rows(tab_s[STAGED:, :], tab_scales)
        nc.sync.dma_start(offsets[:], offs)
        wk_s_raw = tile("wk_s_raw", [P, R], U8)
        load_scale_rows(wk_s_raw[STAGED:, :], wk_scales)
        rows = tile("rows", [P, J + R + N], U8)
        load_scale_rows(rows[STAGED:, J + R :], wv4_scales)
        wq_s_raw = tile("wq_s_raw", [BLOCKS, PASSES, R], U8, AT_WQ_S_RAW)
        nc.sync.dma_start(wq_s_raw[:].bitcast(I32), wq_scales.rearrange("a g w -> g a w").bitcast(I32))
        tab_w = [load_table(0)]
        wv4_c = [load_wv4(0)]

        zero(nc.vector, tab_s[:STAGED, :])
        planes = [tile("planes%d" % a, [P, J + R + N], U8) for a in range(PASSES)]
        for a in range(PASSES):
            zero(nc.vector, planes[a][:])

        deal(rows[STAGED:, J : J + R], wk_s_raw[STAGED:, :], 2, nc.scalar.copy, U32)
        picked_scales = tile("picked_s", [P, J], U8, AT_PICKED_SCALES)
        nc.vector.tensor_copy(picked_scales[:], tab_s[:].indirect(offsets[:]))
        nc.vector.tensor_copy(rows[STAGED:, :J].bitcast(I32), picked_scales[STAGED:, :].bitcast(I32))
        spread_scale_rows(planes[0], rows, STAGED)
        wk_raw = tile("wk_raw", [P, PASSES, R // 2], I32, AT_WK_RAW)
        nc.sync.dma_start(wk_raw[:, 0], wk_words[0].bitcast(I32))
        tab_w.append(load_table(1))
        half = R // 4
        nc.sync.dma_start(wk_raw[:, 1, :half], wk_words[1].bitcast(I32)[:, :half])
        spread_scale_rows(planes[1], rows, STAGED + BLOCKS)
        nc.sync.dma_start(wk_raw[:, 1, half:], wk_words[1].bitcast(I32)[:, half:])

        v_c, v_s = {}, {}

        def gather(a, h, offset=None):
            entries = offsets[:, h * (BANK // LIST_ROWS) : (h + 1) * (BANK // LIST_ROWS)]
            v_s[a, h] = planes[a][:, h * BANK : (h + 1) * BANK]
            v_c[a, h] = tile("v_c%d%d" % (a, h), [P, BANK], U32, offset)
            nc.vector.tensor_copy(v_c[a, h][:], tab_w[a][:].bitcast(U32).indirect(entries))

        gather(0, 0)
        gather(0, 1)
        wq_raw = [load_wq(0)]
        x_raw = [load_f32("x", x, a, AT_X_RAW[a]) for a in range(PASSES)]
        wk_c = [tile("wk_c%d" % a, [P, 2 * R], U8) for a in range(PASSES)]
        deal(wk_c[0][:], wk_raw[:, 0], 4)
        wq_plane = tile("wq_plane", [P, PASSES * R], U8, AT_WQ_PLANE)
        zero(nc.vector, wq_plane[:])
        wq_rows = tile("wq_rows", [BLOCKS, PASSES * R], U8, AT_WQ_ROWS)
        deal(wq_rows[:], wq_s_raw[:].rearrange("p a w -> p (a w)"), 2)
        spread_scale_rows(wq_plane, wq_rows, 0)
        wq_raw.append(load_wq(1))

        def base_pass(out, a, nt, h, cols, start, stop):
            nc.tensor.matmul_mx(
                out=out,
                lhsT=wv4_c[a][:, 2 * nt * P : 2 * (nt + 1) * P].bitcast(FP4X4),
                lhsT_scale=planes[a][:, J + R + nt * P : J + R + (nt + 1) * P],
                rhs=v_c[a, h][:, cols].bitcast(FP8X4),
                rhs_scale=v_s[a, h][:, cols],
                start=start,
                stop=stop,
            )

        partial = {}
        for nt, h in [(nt, 0) for nt in range(N // P)] + [(nt, 1) for nt in reversed(range(N // P))]:
            bank = new_bank([P, BANK])
            base_pass(bank[:], 0, nt, h, slice(0, BANK), True, True)
            partial[nt, h] = tile("partial%d%d" % (nt, h), [P, BANK], F32)
            nc.scalar.copy(partial[nt, h][:], bank[:])

        def key_passes(bank, a, b, h, blk):
            cols = slice(blk * P, (blk + 1) * P)
            for t in range(PACK):
                col = (b * PACK + t) * P
                nc.tensor.matmul_mx(
                    out=bank[:, t, :],
                    lhsT=wk_c[a][:, 2 * col : 2 * (col + P)].bitcast(FP4X4),
                    lhsT_scale=planes[a][:, J + col : J + col + P],
                    rhs=v_c[a, h][:, cols].bitcast(FP8X4),
                    rhs_scale=v_s[a, h][:, cols],
                    start=(a == 0 and t == 0),
                    stop=(a == PASSES - 1 and t == PACK - 1),
                )

        k_banks = {}
        for b in range(PASSES):
            for blk in range(BANK // P):
                k_banks[b, blk] = new_bank([P, PACK, P])
                key_passes(k_banks[b, blk], 0, b, 0, blk)
        gather(1, 0)
        deal(wk_c[1][:, :R], wk_raw[:, 1, :half], 4)
        deal(wk_c[1][:, R:], wk_raw[:, 1, half:], 4)
        gather(1, 1, AT_LAST_WORDS)
        wvd_rows = tile("wvd_raw", [P, PASSES, PACK * N], F32, AT_WVD_RAW)
        nc.sync.dma_start(wvd_rows[:], wvd.rearrange("(a p t) w -> p a (t w)", a=PASSES, t=PACK))
        wvd_raw = [wvd_rows[:, a].rearrange("p (t w) -> p t w", t=PACK) for a in range(PASSES)]
        wv4_c.append(load_wv4(1))
        k_woven = {}
        for b in range(PASSES):
            k_woven[b, 0] = tile("k_woven%d0" % b, [P, BANK, PACK], BF16)
            for blk in range(BANK // P):
                key_passes(k_banks[b, blk], 1, b, 0, blk)
                weave_out_of_bank(k_woven[b, 0], blk, k_banks[b, blk], (b, blk) in KEY_BANKS_ON_VECTOR)
        for b in range(PASSES):
            k_woven[b, 1] = tile("k_woven%d1" % b, [P, BANK, PACK], BF16)
            for blk in range(BANK // P):
                bank = new_bank([P, PACK, P])
                for a in range(PASSES):
                    key_passes(bank, a, b, 1, blk)
                weave_out_of_bank(k_woven[b, 1], blk, bank)

        def deal_wq(b):
            codes = tile("wq_c%d" % b, [P, PASSES, K_PASS], U32, AT_WQ_CODES[b])
            deal(codes[:].rearrange("p a r -> p (a r)"), wq_raw[b][:].rearrange("p a r -> p (a r)"), 8)
            return codes

        wq_c = [deal_wq(0)]
        x_q = [[quantise_part("x0", x_raw[0], part, AT_X_WOVEN[0][part]) for part in range(PARTS)]]
        x_q.append([quantise_part("x1", x_raw[1], 0, AT_X_WOVEN[1][0])])
        wq_c.append(deal_wq(1))
        x_q[1].append(quantise_part("x1", x_raw[1], 1, AT_X_WOVEN[1][1]))

        def query_passes(bank, a, b, blk):
            x_codes, x_plane = x_q[a][blk // 2]
            m_cols = slice(blk % 2 * P, (blk % 2 + 1) * P)
            for t in range(PACK):
                col = a * R + (b * PACK + t) * P
                nc.tensor.matmul_mx(
                    out=bank[:, t, :],
                    lhsT=wq_c[b][:, a, t * P : (t + 1) * P].bitcast(FP8X4),
                    lhsT_scale=wq_plane[:, col : col + P],
                    rhs=x_codes[:, m_cols].bitcast(FP8X4),
                    rhs_scale=x_plane[:, m_cols],
                    start=(a == 0 and t == 0),
                    stop=(a == PASSES - 1 and t == PACK - 1),
                )

        qr_q, wvd_q, kr_q = {}, {}, {}

        def queries(b, part, pass_0_first):
            woven = tile("q_woven%d%d" % (b, part), [P, PART, PACK], BF16, AT_Q_WOVEN[b][part])
            blks = (2 * part, 2 * part + 1)
            banks = {blk: new_bank([P, PACK, P]) for blk in blks}
            if pass_0_first:
                for blk in blks:
                    query_passes(banks[blk], 0, b, blk)
            for blk in blks:
                if not pass_0_first:
                    query_passes(banks[blk], 0, b, blk)
                query_passes(banks[blk], 1, b, blk)
                weave_out_of_bank(woven, blk % 2, banks[blk])
            qr_q[b, part] = quantise("qr%d%d" % (b, part), woven)

        def scores(mt, h):
            bank = new_bank([P, BANK])
            q_cols = slice(mt % 2 * P, (mt % 2 + 1) * P)
            for b in range(PASSES):
                nc.tensor.matmul_mx(
                    out=bank[:],
                    lhsT=qr_q[b, mt // 2][0][:, q_cols].bitcast(FP8X4),
                    lhsT_scale=qr_q[b, mt // 2][1][:, q_cols],
                    rhs=kr_q[b, h][0][:].bitcast(FP8X4),
                    rhs_scale=kr_q[b, h][1][:],
                    start=(b == 0),
                    stop=(b == PASSES - 1),
                )
            res = outs.tile([P, BANK], F32, name="res")
            nc.scalar.activation(res[:], bank[:], COPY, scale=SCORE_SCALE)
            nc.sync.dma_start(out_0[mt * P : (mt + 1) * P, h * BANK : (h + 1) * BANK], res[:])

        def change_pass(bank, a, nt, h, cols):
            codes, plane = wvd_q[a, nt // 2]
            n_cols = slice(nt % 2 * P, (nt % 2 + 1) * P)
            nc.tensor.matmul_mx(
                out=bank[:],
                lhsT=codes[:, n_cols].bitcast(FP8X4),
                lhsT_scale=plane[:, n_cols],
                rhs=v_c[a, h][:, cols].bitcast(FP8X4),
                rhs_scale=v_s[a, h][:, cols],
                start=(a == 0),
                stop=(a == PASSES - 1),
            )

        def values(nt, h, c0=0, width=BANK):
            bank = new_bank([P, width])
            cols = slice(c0, c0 + width)
            change_pass(bank, 0, nt, h, cols)
            base_pass(bank[:], 1, nt, h, cols, False, False)
            change_pass(bank, 1, nt, h, cols)
            res = outs.tile([P, width], F32, name="res")
            nc.vector.tensor_tensor(res[:], bank[:], partial[nt, h][:, cols], ADD)
            nc.sync.dma_start(out_1[nt * P : (nt + 1) * P, h * BANK + c0 : h * BANK + c0 + width], res[:])

        queries(0, 0, True)
        queries(1, 0, False)
        for h in range(HALVES):
            for b in range(PASSES):
                kr_q[b, h] = quantise("kr%d%d" % (b, h), k_woven[b, h], AT_KR_CODES[h][b])
        for b in range(PASSES):
            queries(b, 1, False)

        for h in range(HALVES):
            for mt in range(2):
                scores(mt, h)
        for a in range(PASSES):
            wvd_q[a, 0] = quantise_part("wvd%d" % a, wvd_raw[a], 0, AT_WVD_WOVEN[a][0])
        for h in range(HALVES):
            for mt in range(2, 4):
                scores(mt, h)
            values(0, h)
        for a in range(PASSES):
            wvd_q[a, 1] = quantise_part("wvd%d" % a, wvd_raw[a], 1, AT_WVD_WOVEN[a][1])
        late_tiles = [(nt, h) for nt in range(1, N // P) for h in range(HALVES)]
        for nt, h in late_tiles[: -len(LAST_PIECES)]:
            values(nt, h)
        for (nt, h), pieces in zip(late_tiles[-len(LAST_PIECES) :], LAST_PIECES):
            for c0, width in pieces:
                values(nt, h, c0, width)
